import numpy as np, ml_dtypes
CORES = [40,42,43,45,46]
N = 5
import mx_ref
BF = ml_dtypes.bfloat16
def pick(q, e):
    c = np.concatenate([q[0].reshape(128, -1, 4), np.zeros((128, 1, 4), np.uint8)], axis=1); s = np.concatenate([q[1], np.ones((16, 1), np.uint8)], axis=1)
    return (np.ascontiguousarray(c[:, e].reshape(128, -1)), np.ascontiguousarray(s[:, e]))
def join(*qs):
    return (np.concatenate([q[0] for q in qs], axis=1), np.concatenate([q[1] for q in qs], axis=1))
def put(q, e, v):
    c, s = q[0].reshape(128, -1, 4).copy(), q[1].copy(); c[:, e] = v[0].reshape(128, -1, 4); s[:, e] = v[1]
    return (c.reshape(128, -1), s)
def pk(c, s):
    return (np.ascontiguousarray(c), mx_ref.live(s))
def emit(q):
    return q[0], q[1]
def decode(q):
    o = []
    for b in range(4):
        e = np.zeros((128, 128, 4), np.float32); e[np.arange(128), np.arange(128), b] = 1
        o.append(mx_ref.matmul(mx_ref.quantize(e.reshape(128, 512).astype(BF)), q))
    return np.stack(o, axis=2).reshape(128, -1)
def f(rng, *shape):
    return mx_ref.flush((rng.standard_normal(shape, dtype=np.float32) * np.exp2(rng.integers(-2, 3, shape[:-1] + (1,)))).astype(BF))
def wide(rng, *shape, cols=0):
    v = rng.standard_normal(shape, dtype=np.float32) * np.exp2(rng.integers(-12, 13, shape)).astype(np.float32)
    if cols: v *= np.repeat(np.exp2(rng.integers(-cols, cols + 1, shape[:-2] + (1, shape[-1] // 4))) * (rng.random(shape[:-2] + (1, shape[-1] // 4)) > 0.0625), 4, axis=-1).astype(np.float32)
    return mx_ref.flush(v.astype(BF))
P, K, R = 192, 48, 3
def lift(v):
    v = np.asarray(v).astype(np.float32)
    v[np.abs(v) < np.float32(2.0 ** -16)] = 0
    return v.astype(BF)
def whole(x, hc, u, w):
    i = np.arange(N)
    return {"x": x, "hl": hc[(i - 1) % N], "hc": hc, "hr": hc[(i + 1) % N], "u": u, "w": w}
def query(rng):
    v = np.zeros((N, 128, 512), BF)
    v[:, :, :4] = f(rng, 128, 4)
    return v
def near(rng, hc):
    k = np.repeat(np.exp2(rng.integers(-3, 2, (N, 1, P))), 4, axis=2)
    return lift(hc.astype(np.float32) + f(rng, N, 128, 4 * P).astype(np.float32) * k)
def setup_inputs(rng):
    hc = lift(f(rng, N, 128, 4 * P))
    return whole(near(rng, hc), hc, query(rng), f(rng, N, 128, 512))
def setup_inputs_spread(rng):
    hc = lift(wide(rng, N, 128, 4 * P, cols=4))
    return whole(lift(wide(rng, N, 128, 4 * P, cols=4)), hc, query(rng), f(rng, N, 128, 512))
def setup_inputs_ties(rng):
    d = setup_inputs(rng)
    g = rng.permutation(P) // 7
    s = np.repeat(1 - 2 * rng.integers(0, 2, P), 4).astype(np.float32)
    def same(v):
        return (v.reshape(N, 128, P, 4)[:, :, g].reshape(N, 128, 4 * P).astype(np.float32) * s).astype(BF)
    return whole(same(d["x"]), same(d["hc"]), d["u"], d["w"])
def setup_inputs_again(rng):
    d = setup_inputs(rng)
    k = np.ones(P, np.float32)
    k[rng.permutation(P)[:K]] = 1024
    k = np.repeat(k, 4)
    return whole(lift(d["x"].astype(np.float32) * k), lift(d["hc"].astype(np.float32) * k), d["u"], d["w"])
def setup_inputs_still(rng):
    d = setup_inputs(rng)
    v = rng.integers(128, 256, (16, 8, P, 4)) * np.exp2(rng.integers(-10, -7, (16, 8, P, 4)))
    v[:, 0, :, 0] = (128 + 8 * np.argsort(rng.random((16, P)), axis=0) + rng.integers(1, 8, (16, P))) * 2.0 ** -7
    v = v * rng.choice([-1.0, 1.0], v.shape) * np.exp2(rng.integers(-2, 3, (16, 1, P, 1)))
    v = v.reshape(128, 4 * P).astype(np.float32).astype(BF)
    held = decode(mx_ref.quantize(v)).astype(BF)
    s = int(rng.integers(0, N))
    hc = np.array(d["hc"])
    for r in range(s - 1, s + 3): hc[r % N] = v
    x = near(rng, hc)
    x[s] = held
    few = np.array(x[(s + 1) % N]).reshape(128, P, 4)
    rest = rng.permutation(P)[K // 2:]
    few[:, rest] = held.reshape(128, P, 4)[:, rest]
    x[(s + 1) % N] = few.reshape(128, 4 * P)
    return whole(x, hc, d["u"], d["w"])
def setup_inputs_one(rng):
    d = setup_inputs(rng)
    p, t = int(rng.integers(0, 128)), int(rng.integers(0, 4))
    u = np.zeros((N, 128, 512), BF)
    u[:, p, t] = -1.5
    off = np.sort(rng.permutation(P)[K // 2:])
    x, hc = np.array(d["x"]).reshape(N, 128, P, 4), np.array(d["hc"]).reshape(N, 128, P, 4)
    x[:, :, off[::2]] = (x[:, :, off[::2]].astype(np.float32) - np.float32(128)).astype(BF)
    x[:, p, off, t] = 0
    hc[:, p, off, t] = 0
    return whole(x.reshape(N, 128, 4 * P), hc.reshape(N, 128, 4 * P), u, d["w"])
def check_inputs(d):
    b = []
    for k, lo, hi in (("x", -16, 24), ("hl", -16, 24), ("hc", -16, 24), ("hr", -16, 24), ("u", -30, 30), ("w", -30, 30)):
        v = np.abs(d[k].astype(np.float32))
        if not (np.isfinite(v).all() and ((v == 0) | (v >= 2.0 ** lo) & (v <= 2.0 ** hi)).all()): b.append("a value of " + k)
    i = np.arange(N)
    hl, hc, hr, u = [d[k].astype(np.float32) for k in ("hl", "hc", "hr", "u")]
    if (hl != hc[(i - 1) % N]).any(): b.append("hl isn't the left neighbour's hc")
    if (hr != hc[(i + 1) % N]).any(): b.append("hr isn't the right neighbour's hc")
    if (u != u[:1]).any(): b.append("u isn't the same on all ranks")
    if (d["u"][:, :, 4:].astype(np.float32) != 0).any(): b.append("u has numbers behind its column 0")
    return b
def reference(x, hl, hc, hr, u, w):
    a, h, b = [[mx_ref.quantize(np.ascontiguousarray(v[r])) for r in range(N)] for v in (hl, hc, hr)]
    s = [x[r] for r in range(N)]
    ch = np.zeros((N, R, K), np.float32)
    for t in range(R):
        dh = decode(join(*h)).reshape(128, N, 4 * P).transpose(1, 0, 2)
        at, dq = [], []
        for r in range(N):
            v = ((dh[(r - 1) % N] + dh[(r + 1) % N]) - dh[r] * np.float32(2)) * np.float32(0.25)
            s[r] = (s[r].astype(np.float32) + v).astype(BF)
            q = mx_ref.quantize(np.ascontiguousarray((s[r].astype(np.float32) - dh[r]).astype(BF)))
            z = np.abs(mx_ref.matmul(mx_ref.quantize(np.ascontiguousarray(u[r])), q)[0]) + np.float32(0)
            e = np.argsort(-z, kind="stable")[:K]
            ch[r, t] = e
            at.append(e)
            dq.append(pick(q, e))
        dd = decode(join(*dq)).reshape(128, N, K, 4)
        for r in range(N):
            v = mx_ref.quantize(np.ascontiguousarray((dh[r].reshape(128, P, 4)[:, at[r]] + dd[:, r]).reshape(128, -1).astype(BF)))
            for held, o in ((a, (r + 1) % N), (h, r), (b, (r - 1) % N)): held[o] = put(held[o], at[r], v)
    oc, osc = np.zeros((N, 128, 12 * P), np.uint8), np.zeros((N, 16, 3 * P), np.uint8)
    y = np.zeros((N, 128, P), np.float32)
    for r in range(N):
        oc[r], osc[r] = emit(join(a[r], h[r], b[r]))
        y[r] = mx_ref.matmul(mx_ref.quantize(np.ascontiguousarray(w[r])), a[r])
    return {"oc": oc, "osc": osc, "xe": np.stack(s).astype(np.float32), "ch": ch, "y": y}

@@ -1,0 +1,301 @@
+from concourse.bass import DstId, RemoteDMATransfer
+from concourse.mybir import dt, AluOpType as OP, AxisListType, ActivationFunctionType as AF
+
+P, K, R = 192, 48, 3
+BF, F32, I32, U16, FP8, U8 = "bfloat16", "float32", "int32", "uint16", "float8_e4m3fn_x4", "uint8"
+SND = P + K + 12
+STEPS = "x0 x1 d0 x2 d1 x3 d2 d3"
+
+SCRATCH = {}
+SCRATCH.update({n: ("sbuf", [128, w], BF) for n, w in dict(
+    x0=768, x1=768, x2=768, x3=768, tl=768, tc=768, tr=768, tu=4, tw=512, ub=512, ones=128, ident=128, z128=128, stage=2048,
+    cet=512, cst=512, thr=192, k96=96, k192=192, dtile=768, stile=768, g0=208, g1=208, ot=512, xt=512).items()})
+SCRATCH.update({n: ("sbuf", [128, w], F32) for n, w in dict(
+    lf=1, hf=1, h1=1, jc=1, cz=4, row16=12, bm=12, below=12, above=12, sab=192, nsc=2, df=192, rr=2, xf=12, etr=96,
+    chs=R * K, xout=768, yout=192).items()})
+SCRATCH.update({n: ("sbuf", [128, w], I32) for n, w in dict(pint=1, lint=1, am=128, am15=128).items()})
+_Q = dict(uq=128, wq=128, e1=512, eq=512, em=512, ce=128, cs=128, dq=P, oq=128, fin=3 * P)
+for _t in range(R):
+    _Q.update({"wA%d" % _t: SND, "wB%d" % _t: SND, "wH%d" % _t: P + K + 128, "sq%d" % _t: P})
+    SCRATCH["eo%d" % _t] = ("sbuf", [128, 4], U16)
+    for _n in "AHB":
+        SCRATCH["so%s%d" % (_n, _t)] = ("sbuf", [128, 12], U16)
+for _n, _w in _Q.items():
+    SCRATCH[_n] = ("sbuf", [128, _w], FP8)
+    SCRATCH[_n + "_s"] = ("sbuf", [128, _w], U8)
+for _b in range(4):
+    SCRATCH["psZ%d" % _b] = ("psum", [128, 512], F32)
+    SCRATCH["psH%d" % _b] = ("psum", [128, 512], F32)
+
+SEMAPHORES = (["sv", "sa", "st", "sg", "left", "lc", "ll", "lr", "lx", "lu", "lw", "out"]
+              + ["rA%d" % t for t in range(R)] + ["rB%d" % t for t in range(R)])
+
+
+def rank_program(g, core, T, topo):
+    rank = T.rank_of(core)
+    if rank is None:
+        return
+    n = len(T.cores)
+    right, left = T.cores[(rank + 1) % n], T.cores[(rank - 1) % n]
+    Q = {"v": g.vector, "a": g.scalar, "t": g.tensor, "g": g, "s": g.sync}
+    cnt = {"v": 0, "a": 0, "t": 0, "g": 0}
+    seen = {q: {} for q in Q}
+    total = {"out": 0, "left": 0}
+
+    def wait(q, deps):
+        need = {}
+        for s, v in deps:
+            need[s] = max(v, need.get(s, 0))
+        for s, v in need.items():
+            if seen[q].get(s, 0) < v:
+                Q[q].wait_ge(T.sem[s], v)
+                seen[q][s] = v
+
+    CALLS = {"act": g.scalar.activation, "mm": g.tensor.matmul_mx, "quant": g.vector.quantize_mx, "copy": g.vector.tensor_copy,
+             "tt": g.vector.tensor_tensor, "ts": g.vector.tensor_scalar, "red": g.vector.tensor_reduce,
+             "tr": g.vector.transpose, "fill": g.vector.memset, "iota": g.iota, "select": g.affine_select}
+    QUEUE = {"act": "a", "mm": "t", "iota": "g", "select": "g"}
+
+    def run(name, deps, *args, **kw):
+        q = QUEUE.get(name, "v")
+        wait(q, deps)
+        CALLS[name](*args, **kw).then_inc(T.sem["s" + q], 1)
+        cnt[q] += 1
+        return ("s" + q, cnt[q])
+
+    def load(q, sem, out, in_):
+        Q[q].dma_start(out, in_).then_inc(T.sem[sem], 16)
+        return (sem, 16)
+
+    def store(q, deps, out, in_):
+        wait(q, deps)
+        Q[q].dma_start(out, in_).then_inc(T.sem.out, 16)
+        total["out"] += 16
+
+    def ts(deps, out, in0, s1, op0, s2=None, op1=None):
+        kw = {} if op1 is None else {"op1": op1}
+        return run("ts", deps, out=out, in0=in0, scalar1=s1, scalar2=s2, op0=op0, **kw)
+
+    def cols(name, a, b):
+        return T[name][:, a:b], T[name + "_s"][:, a:b]
+
+    def win(k, t, a, b):
+        o = P * "AHB".index(k)
+        return cols("fin", o + a, o + b) if t == R else cols("w%s%d" % (k, t), a, b)
+
+    def mm(deps, out, l, r, start=True, stop=True):
+        return run("mm", deps, out, l[0], l[1], r[0], r[1], start, stop)
+
+    def quant(deps, q, tile):
+        return run("quant", deps, q[0], q[1], tile)
+
+    psZ = [T["psZ%d" % b] for b in range(4)]
+    psH = [T["psH%d" % b] for b in range(4)]
+    XS = [T.x0, T.x1, T.x2, T.x3]
+    U, DQ, CE, CS, OQ = cols("uq", 0, 128), cols("dq", 0, P), cols("ce", 0, 128), cols("cs", 0, 128), cols("oq", 0, 128)
+    E = {c: [cols(c, 128 * b, 128 * b + 128) for b in range(4)] for c in ("e1", "eq", "em")}
+    row = [slice(b, 4 * P, 4) for b in range(4)]
+
+    ll = load("a", "ll", T.tl[:], T.hl[:])
+    lc = load("s", "lc", T.tc[:], T.hc[:])
+    lu = load("s", "lu", T.tu[:], T.u[:, 0:4])
+    lr = load("s", "lr", T.tr[:], T.hr[:])
+    lx = load("a", "lx", T.x0[:], T.x[:])
+    lw = load("s", "lw", T.tw[:], T.w[:])
+
+    small = {"allow_small_or_imprecise_dtypes": True}
+    c_ones = run("fill", [], T.ones[:], 1.0)
+    i_p = run("iota", [], T.pint[:], [[0, 1]], 0, 1)
+    c_id = run("select", [c_ones], T.ident[:], T.ones[:], [[-1, 128]], OP.is_equal, 0.0, 0, 1)
+    c_stage = run("fill", [], T.stage[:], 0.0)
+    c_z = run("fill", [], T.z128[:], 0.0)
+    i_am = run("iota", [], T.am[:], [[1, 128]], 128, -1)
+    i_k = run("iota", [], T.k96[:], [[16, 3], [0, 2], [1, 16]], P, 0, **small)
+    i_r = run("iota", [], T.row16[:], [[16, 12]], 0, 0, **small)
+    tiny = -(2.0 ** -120)
+    i_t0 = run("select", [c_z], T.thr[:, 0:128], T.z128[:], [[1, 128]], OP.is_ge, tiny, 0, -1)
+    i_t1 = run("select", [c_z], T.thr[:, 128:P], T.z128[:, 0:64], [[1, 64]], OP.is_ge, tiny, 64, -1)
+
+    def diag(c, before):
+        return [ts([c_id, c_stage] + before, T.stage[:, 512 * b + b:512 * (b + 1):4], T.ident[:], c, OP.mult) for b in range(4)]
+
+    def pack(name, d):
+        return quant(d, cols(name, 0, 512), T.stage[:])
+
+    u4 = [run("act", [lu, c_z], T.ub[:, t:512:4], T.z128[:], AF.Identity, bias=T.tu[:, t:t + 1]) for t in range(4)]
+    d = diag(0.25, [])
+    v_l = ts([i_p], T.lint[:], T.pint[:], 15, OP.bitwise_and)
+    v_j = run("copy", [i_p], T.jc[:], T.pint[:])
+    v_cz = run("fill", [], T.cz[:], 0.0)
+    k_eq = pack("eq", d)
+    v_lf = run("copy", [v_l], T.lf[:], T.lint[:])
+    v_am = ts([i_am], T.am15[:], T.am[:], 15, OP.bitwise_and)
+    d = diag(1.0, [k_eq])
+    v_hf = run("tt", [v_lf, v_j], T.hf[:], T.jc[:], T.lf[:], OP.subtract)
+    v_z = [run("copy", [v_cz, v_lf], T.cz[:, 2:3], T.lf[:]),
+           run("copy", [v_cz, v_lf], T.cz[64:128, 3:4], T.lf[64:128, :])]
+    k_e1 = pack("e1", d)
+    v_h1 = ts([v_hf], T.h1[:], T.hf[:], 64.0, OP.add)
+    sh = {"A": [quant([ll], win("A", 0, 0, P), T.tl[:])], "H": [quant([lc], win("H", 0, 0, P), T.tc[:])]}
+    d = diag(-0.5, [k_e1])
+    v_z += [run("copy", [v_cz, v_hf], T.cz[:, 0:1], T.hf[:]),
+            run("copy", [v_cz, v_h1], T.cz[64:128, 1:2], T.h1[64:128, :])]
+    k_em = pack("em", d)
+    sh["B"] = [quant([lr], win("B", 0, 0, P), T.tr[:])]
+    v_e = [run("act", [c_z] + v_z, T.cet[:, t:512:4], T.z128[:], AF.Identity, bias=T.cz[:, t:t + 1]) for t in range(4)]
+    k_u = quant(u4, U, T.ub[:])
+
+    free = {(k, b): [] for b in range(4) for k in "ZH"}
+
+    def decode_h(t):
+        return [mm(sh["H"] + free["H", b] + [k_e1], psH[b][:, 0:P], E["e1"][b], win("H", t, 0, P)) for b in range(4)]
+
+    def decode_a(t):
+        for b in range(4):
+            mm(sh["A"] + free["Z", b] + [k_eq], psZ[b][:, 0:P], E["eq"][b], win("A", t, 0, P), True, False)
+
+    def decode_bh(t):
+        z = []
+        for b in range(4):
+            mm(sh["B"], psZ[b][:, 0:P], E["eq"][b], win("B", t, 0, P), False, False)
+            z.append(mm([k_em], psZ[b][:, 0:P], E["em"][b], win("H", t, 0, P), False, True))
+        return z
+
+    decode_a(0)
+    tH = decode_h(0)
+    tZ = decode_bh(0)
+
+    def send(deps, src, to_right, to_left, t):
+        wait("g", deps)
+        tr = []
+        for who, dst, sem, odd in ((right, to_right, "rA%d" % t, 0), (left, to_left, "rB%d" % t, 1)):
+            rid, pid, _ = topo.addr(who)
+            eng = topo.engines(core, who)[odd::2]
+            tr.append(RemoteDMATransfer(dst_ids=[DstId(rid=rid, pnc=pid)], dma_engine_mask=sum(1 << e for e in eng),
+                                        remote_sem=T.sem[sem], src=src, dst=dst))
+            total["left"] += len(eng)
+        g.remote_dma_fused(tr, local_sem=T.sem.left)
+
+    got = {"A": 2 * len(topo.engines(left, core)[0::2]), "B": 2 * len(topo.engines(right, core)[1::2])}
+    chtok = []
+
+    for t in range(R):
+        last = t == R - 1
+        tx, td = {}, {}
+        for step in STEPS.split():
+            b = int(step[1])
+            x = XS[t + 1][:, row[b]]
+            if step[0] == "x":
+                tx[b] = run("tt", [tZ[b], lx], x, psZ[b][:, 0:P], XS[t][:, row[b]], OP.add)
+            else:
+                td[b] = run("tt", [tx[b], tH[b]], T.dtile[:, row[b]], x, psH[b][:, 0:P], OP.subtract)
+        tq = quant(list(td.values()), DQ, T.dtile[:])
+        for b in range(4):
+            mm([tx[b]], psZ[b][:, 0:P], E["e1"][b], win("H", t, 0, P), True, False)
+        mr = mm([tq, k_u], psH[0][:, 0:P], U, DQ)
+        mc0 = mm([tq], psH[1][:, 0:128], cols("dq", 0, 128), U)
+        mc1 = mm([tq], psH[2][:, 0:128], cols("dq", 64, 192), U)
+        mS = [mm([tq], psZ[b][:, 0:P], E["e1"][b], DQ, False, True) for b in range(4)]
+
+        def minus(m, bank, h):
+            return run("red", [m], T.nsc[:, h:h + 1], bank[:, 0:2], AxisListType.X, OP.max, negate=True,
+                       apply_absolute_value=True)
+
+        if t == 0:
+            v_f = [run("fill", [], T.g0[:, P:P + 16], float(P)), run("fill", [], T.g1[:, P:P + 16], float(P)),
+                   run("fill", [], T.ot[:, 384:512], 0.0)]
+            v_k = [run("copy", [i_k], T.k192[:, h:192:2], T.k96[:]) for h in range(2)]
+            k_ce = [quant(v_e, CE, T.cet[:])]
+        n0, n1 = T.nsc[:, 0:1], T.nsc[:, 1:2]
+        aA = [run("act", [mr], T.sab[:, c:e], psH[0][:, c:e], AF.Abs) for c, e in ((0, 128), (128, P))]
+        aS = [run("act", [mS[b]], T.stile[:, row[b]], psZ[b][:, 0:P], AF.Copy) for b in range(4)]
+        if last:
+            axo = run("act", list(tx.values()), T.xout[:], XS[R][:], AF.Copy)
+            store("s", [axo], T.xe[:], T.xout[:])
+        vc0 = minus(mc0, psH[1], 0)
+        vc1 = minus(mc1, psH[2], 1)
+        vd0 = ts([aA[0], vc0], T.df[:, 0:128], T.sab[:, 0:128], n0, OP.add)
+        vi1 = ts([aA[0], vc1], T.g1[:, 0:128], T.sab[:, 0:128], n1, OP.add, 0.0, OP.is_ge)
+        vd1 = ts([aA[1], vc1], T.df[:, 128:P], T.sab[:, 128:P], n1, OP.add)
+        vi0 = ts([aA[1], vc0], T.g0[:, 128:P], T.sab[:, 128:P], n0, OP.add, 0.0, OP.is_gt)
+        vg0 = run("tt", [vd0, i_t0], T.g0[:, 0:128], T.df[:, 0:128], T.thr[:, 0:128], OP.is_gt)
+        vg1 = run("tt", [vd1, i_t1], T.g1[:, 128:P], T.df[:, 128:P], T.thr[:, 128:P], OP.is_gt)
+        if t == 0:
+            v_b = [ts([i_r, v_hf], T.bm[:, 0:8], T.row16[:, 0:8], T.hf[:], OP.is_equal),
+                   ts([i_r, v_h1], T.bm[:, 8:12], T.row16[:, 8:12], T.h1[:], OP.is_equal)]
+        vr0 = run("red", [vg0, vi0] + v_f, T.rr[:, 0:1], T.g0[:, 0:P + 1], AxisListType.X, OP.add)
+        vr1 = run("red", [vg1, vi1] + v_f, T.rr[:, 1:2], T.g1[:, 0:P + 1], AxisListType.X, OP.add)
+        if t == 0:
+            v_b = [ts(v_b, T.below[:], T.bm[:], float(P + K), OP.mult),
+                   ts(v_b, T.above[:], T.bm[:], P + K - 1000000.0, OP.mult, 1000000.0, OP.add),
+                   run("fill", [], T.xt[:], 0.0)]
+        r0, r1 = T.rr[:, 0:1], T.rr[:, 1:2]
+        vo0 = ts([vr0] + v_k, T.ot[:, 0:384:2], T.k192[:], r0, OP.is_equal)
+        vx = [ts([vr0] + v_b, T.xf[:, 0:8], T.below[:, 0:8], r0, OP.is_gt, r0, OP.mult)]
+        vo1 = ts([vr1] + v_k, T.ot[:, 1:384:2], T.k192[:], r1, OP.is_equal)
+        vx.append(ts([vr1] + v_b, T.xf[:, 8:12], T.below[:, 8:12], r1, OP.is_gt, r1, OP.mult))
+        vj = [ts([vr0] + v_b, T.xt[:, e:32:4], T.above[:, 0:8], r0, OP.is_le, c[:], OP.mult) for e, c in ((1, T.hf), (3, T.lf))]
+        vqo = quant([vo0, vo1], OQ, T.ot[:])
+        me = mm([vqo] + k_ce, psH[3][:, 0:128], CE, OQ)
+        S, eo = cols("sq%d" % t, 0, P), T["eo%d" % t]
+        big = 1.5 * 2.0 ** 27
+        vh = ts(vx, T.xt[:, 0:48:4], T.xf[:], big, OP.add, big, OP.subtract)
+        vj += [ts([vr1], T.xt[:, 32 + e:48:4], T.above[:, 8:12], r1, OP.is_le, c[:], OP.mult) for e, c in ((1, T.h1), (3, T.lf))]
+        vl = run("tt", [vh], T.xt[:, 2:48:4], T.xf[:], T.xt[:, 0:48:4], OP.subtract)
+        vqs = quant(aS, S, T.stile[:])
+        H, X, msg = win("H", t, P, P + K), win("H", t, P + K, P + K + 128), win("H", t, P, SND)
+        ve = run("tr", [me], T.etr[:], psH[3][:, 0:96])
+        vqx = quant([vl, vh] + vj, X, T.xt[:])
+        veo = run("copy", [ve], eo[:, 0:3], T.etr[:, 0:96:32])
+        vp = run("copy", [veo, vqs], H[0].bitcast(dt.uint32), S[0].bitcast(dt.uint32).indirect(eo[:, 0:3]))
+        ap = run("act", [veo, vqs], H[1], S[1].indirect(eo[:, 0:3]), AF.Copy)
+        da, db = win("A", t, P, SND), win("B", t, P, SND)
+        send([vp, vqx], msg[0].bitcast(dt.uint8), da[0].bitcast(dt.uint8), db[0].bitcast(dt.uint8), t)
+        send([ap, vqx], msg[1], da[1], db[1], t)
+        ach = [run("act", [ve], T.chs[0:1, K * t + 16 * m:K * t + 16 * m + 16], psH[3][0:1, 32 * m:32 * m + 16], AF.Copy)
+               for m in range(3)]
+        chtok.append(ach[-1])
+        if t == 0:
+            v_c = [ts([v_am], T.cst[:, h:512:4], T.am15[:], 0.0, OP.is_equal) for h in range(4)]
+            k_cs = quant(v_c, CS, T.cst[:])
+
+        def places(k, deps, bank, tile, c):
+            m = mm(deps + [k_cs], bank[:, 0:128], CS, tile)
+            return lambda: run("copy", [m], T["so%s%d" % (k, t)][:], bank[:, c:c + 12])
+
+        def pick(k, deps):
+            so, d, w = T["so%s%d" % (k, t)], win(k, t + 1, 0, P), cols("w%s%d" % (k, t), 0, SND)
+            return [run("copy", deps, d[0].bitcast(dt.uint32), w[0].bitcast(dt.uint32).indirect(so[:])),
+                    run("act", deps, d[1], w[1].indirect(so[:]), AF.Copy)]
+
+        vsh = places("H", [vqx, aS[0]], psZ[0], X, 0)()
+        sh["H"] = pick("H", [vsh, vp, ap])
+        for b, d in enumerate((aA, [vc0], [vc1], ach + [ve])):
+            free["H", b] = d
+        if not last:
+            tH = decode_h(t + 1)
+        else:
+            k_w = quant([lw], cols("wq", 0, 128), T.tw[:])
+            store("s", chtok, T.ch[:], T.chs[0:1, :])
+            store("s", sh["H"], T.oc[:, 4 * P:8 * P], T.fin[:, P:2 * P].bitcast(dt.uint8))
+        ra, rb = ("rA%d" % t, got["A"]), ("rB%d" % t, got["B"])
+        la = places("A", [ra, aS[2]], psZ[2], win("A", t, SND - 128, SND), 116)
+        lb = places("B", [rb, aS[3]], psZ[3], win("B", t, SND - 128, SND), 116)
+        vsa = la()
+        sh["A"] = pick("A", [vsa, ra])
+        vsb = lb()
+        sh["B"] = pick("B", [vsb, rb])
+        for b, d in enumerate((vsh, aS[1], vsa, vsb)):
+            free["Z", b] = [d]
+        if not last:
+            decode_a(t + 1)
+            tZ = decode_bh(t + 1)
+
+    my = mm(sh["A"] + free["Z", 0] + [k_w], psZ[0][:, 0:P], cols("wq", 0, 128), win("A", R, 0, P))
+    vy = run("copy", [my], T.yout[:], psZ[0][:, 0:P])
+    store("s", sh["A"], T.oc[:, 0:4 * P], T.fin[:, 0:P].bitcast(dt.uint8))
+    store("s", sh["B"], T.oc[:, 8 * P:12 * P], T.fin[:, 2 * P:3 * P].bitcast(dt.uint8))
+    for k in range(4):
+        store("a" if k % 2 else "s", sh["A"] + sh["B"] + sh["H"], T.osc[4 * k:4 * k + 4, :], T.fin_s[32 * k:32 * k + 4, :])
+    store("a", [vy], T.y[:], T.yout[:])
+    wait("g", [("s" + q, c) for q, c in cnt.items()] + list(total.items()))

@@ -1,23 +1,30 @@
 from concourse.bass import DstId, RemoteDMATransfer
-from concourse.mybir import dt, AluOpType as OP, AxisListType, ActivationFunctionType as AF
+from concourse.mybir import dt, AluOpType as OP, ActivationFunctionType as AF
 
 P, K, R = 192, 48, 3
-BF, F32, I32, U16, FP8, U8 = "bfloat16", "float32", "int32", "uint16", "float8_e4m3fn_x4", "uint8"
+L = 128
+BF, F32, U16, FP8, U8 = "bfloat16", "float32", "uint16", "float8_e4m3fn_x4", "uint8"
 SND = P + K + 12
-STEPS = "x0 x1 d0 x2 d1 x3 d2 d3"
+N0, N1 = L + P, L + P + P + P - L
+NE = 51
+DRIFT = "x0L x0R x1L d0L x1R x2L d1L x3L d2L d3L x2R x3R qL d0R d1R d2R d3R qR"
+RANKS = "eq0 gt0 sL0 ge1 gR0 eq1 gt1 sR0 s1"
+LISTS = "o0 a0 o1 a1 b0 qo hi b1 lo es qs eo pick"
+FIRST = "A0 A1 A2 A3 B0 B1 B2 B3 H0 H1 h0 H2 h1 H3 h2 h3"
+LATER = "A0 A1 A2 B0 H0 B1 H1 B2 H2 A3 B3 H3"
 
 SCRATCH = {}
 SCRATCH.update({n: ("sbuf", [128, w], BF) for n, w in dict(
-    x0=768, x1=768, x2=768, x3=768, tl=768, tc=768, tr=768, tu=4, tw=512, ub=512, ones=128, ident=128, z128=128, stage=2048,
-    cet=512, cst=512, thr=192, k96=96, k192=192, dtile=768, stile=768, g0=208, g1=208, ot=512, xt=512).items()})
+    x0=768, x1=768, x2=768, x3=768, tl=768, tc=768, tr=768, tu=4, tw=512, ub=512, idx=128, stq=516, stm=516, st1=516,
+    cet=512, cst=512, i16=512, k51=NE, kq=2 * NE, dtile=1024, stile=4 * (P + 12), cmp=N1, mul=N1, acc=N1, ot=512,
+    ini=2, hf=2, h1=2).items()})
 SCRATCH.update({n: ("sbuf", [128, w], F32) for n, w in dict(
-    lf=1, hf=1, h1=1, jc=1, cz=4, row16=12, bm=12, below=12, above=12, sab=192, nsc=2, df=192, rr=2, xf=12, etr=96,
-    chs=R * K, xout=768, yout=192).items()})
-SCRATCH.update({n: ("sbuf", [128, w], I32) for n, w in dict(pint=1, lint=1, am=128, am15=128).items()})
-_Q = dict(uq=128, wq=128, e1=512, eq=512, em=512, ce=128, cs=128, dq=P, oq=128, fin=3 * P)
+    npc=1, c16=8, s16=8, junk=8, bm=8, hp=1, lf=1, nlf=1, th=2, below=8, above=8, sab=192, aj=2, xf=12,
+    i17=NE, m1=NE, m2=NE, me=NE, es=NE, chs=R * K, xout=768, yout=192).items()})
+SCRATCH["eo"] = ("sbuf", [128, 4], U16)
+_Q = dict(uq=128, wq=128, e1=512, eq=512, em=512, ce=128, cs=128, dq=256, oq=128, fin=3 * P)
 for _t in range(R):
-    _Q.update({"wA%d" % _t: SND, "wB%d" % _t: SND, "wH%d" % _t: P + K + 128, "sq%d" % _t: P})
-    SCRATCH["eo%d" % _t] = ("sbuf", [128, 4], U16)
+    _Q.update({"wA%d" % _t: SND, "wB%d" % _t: SND, "wH%d" % _t: P + 64, "sq%d" % _t: P + 12})
     for _n in "AHB":
         SCRATCH["so%s%d" % (_n, _t)] = ("sbuf", [128, 12], U16)
 for _n, _w in _Q.items():
@@ -52,8 +59,8 @@ def rank_program(g, core, T, topo):
                 seen[q][s] = v
 
     CALLS = {"act": g.scalar.activation, "mm": g.tensor.matmul_mx, "quant": g.vector.quantize_mx, "copy": g.vector.tensor_copy,
-             "tt": g.vector.tensor_tensor, "ts": g.vector.tensor_scalar, "red": g.vector.tensor_reduce,
-             "tr": g.vector.transpose, "fill": g.vector.memset, "iota": g.iota, "select": g.affine_select}
+             "tt": g.vector.tensor_tensor, "ts": g.vector.tensor_scalar, "scan": g.vector.tensor_tensor_scan,
+             "fill": g.vector.memset, "iota": g.iota, "select": g.affine_select}
     QUEUE = {"act": "a", "mm": "t", "iota": "g", "select": "g"}
 
     def run(name, deps, *args, **kw):
@@ -76,6 +83,12 @@ def rank_program(g, core, T, topo):
         kw = {} if op1 is None else {"op1": op1}
         return run("ts", deps, out=out, in0=in0, scalar1=s1, scalar2=s2, op0=op0, **kw)
 
+    def lin(deps, out, in_, scale=1.0, bias=0.0):
+        return run("act", deps, out, in_, AF.Identity, bias=bias, scale=scale)
+
+    def iota(out, pattern, base, step):
+        return run("iota", [], out, pattern, base, step, allow_small_or_imprecise_dtypes=True)
+
     def cols(name, a, b):
         return T[name][:, a:b], T[name + "_s"][:, a:b]
 
@@ -91,79 +104,86 @@ def rank_program(g, core, T, topo):
 
     psZ = [T["psZ%d" % b] for b in range(4)]
     psH = [T["psH%d" % b] for b in range(4)]
+    psS = [psZ[2], psZ[3], psH[2], psH[3]]
     XS = [T.x0, T.x1, T.x2, T.x3]
     U, DQ, CE, CS, OQ = cols("uq", 0, 128), cols("dq", 0, P), cols("ce", 0, 128), cols("cs", 0, 128), cols("oq", 0, 128)
     E = {c: [cols(c, 128 * b, 128 * b + 128) for b in range(4)] for c in ("e1", "eq", "em")}
-    row = [slice(b, 4 * P, 4) for b in range(4)]
+    up = 2.0 ** 40
 
-    ll = load("a", "ll", T.tl[:], T.hl[:])
+    ll = load("s", "ll", T.tl[:], T.hl[:])
+    lu = load("a", "lu", T.tu[:], T.u[:, 0:4])
+    lr = load("a", "lr", T.tr[:], T.hr[:])
     lc = load("s", "lc", T.tc[:], T.hc[:])
-    lu = load("s", "lu", T.tu[:], T.u[:, 0:4])
-    lr = load("s", "lr", T.tr[:], T.hr[:])
-    lx = load("a", "lx", T.x0[:], T.x[:])
-    lw = load("s", "lw", T.tw[:], T.w[:])
+    lx = load("s", "lx", T.x0[:], T.x[:])
 
-    small = {"allow_small_or_imprecise_dtypes": True}
-    c_ones = run("fill", [], T.ones[:], 1.0)
-    i_p = run("iota", [], T.pint[:], [[0, 1]], 0, 1)
-    c_id = run("select", [c_ones], T.ident[:], T.ones[:], [[-1, 128]], OP.is_equal, 0.0, 0, 1)
-    c_stage = run("fill", [], T.stage[:], 0.0)
-    c_z = run("fill", [], T.z128[:], 0.0)
-    i_am = run("iota", [], T.am[:], [[1, 128]], 128, -1)
-    i_k = run("iota", [], T.k96[:], [[16, 3], [0, 2], [1, 16]], P, 0, **small)
-    i_r = run("iota", [], T.row16[:], [[16, 12]], 0, 0, **small)
-    tiny = -(2.0 ** -120)
-    i_t0 = run("select", [c_z], T.thr[:, 0:128], T.z128[:], [[1, 128]], OP.is_ge, tiny, 0, -1)
-    i_t1 = run("select", [c_z], T.thr[:, 128:P], T.z128[:, 0:64], [[1, 64]], OP.is_ge, tiny, 64, -1)
+    i_idx = iota(T.idx[:], [[1, 128]], 0, -1)
+    i_c = iota(T.c16[:], [[0, 8]], 16, 0)
+    i_p = iota(T.npc[:], [[0, 1]], -16, -1)
+    i_s = run("select", [i_c], T.s16[:], T.c16[:], [[-16, 8]], OP.is_ge, 0.0, 0, 1)
+    i_k = iota(T.k51[:], [[16, 3], [1, 17]], P - 1, 0)
+    i_bm = run("select", [i_s], T.bm[:], T.s16[:], [[16, 8]], OP.is_ge, 0.0, 15, -1)
+    i_k = run("select", [i_k], T.k51[:], T.k51[:], [[0, 3], [1, 17]], OP.is_gt, -64.0, 0, 0)
+    i_17 = iota(T.i17[:], [[0, 3], [1, 17]], -1, 0)
+    i_zd = iota(T.dtile[:, 4 * P:], [[0, 1024 - 4 * P]], 0, 0)
+    i_m = iota(T.mul[:], [[0, N1]], 1, 0)
+    i_zo = iota(T.ot[:, 4 * NE:], [[0, 512 - 4 * NE]], 0, 0)
+    i_m = [run("select", [i_m], T.mul[:, 0:L], T.mul[:, 0:L], [[1, L]], OP.not_equal, up, 0, -1),
+           run("select", [i_m], T.mul[:, N0:N0 + 64], T.mul[:, N0:N0 + 64], [[1, 64]], OP.not_equal, up, 64, -1)]
+    i_zx = iota(T.stile[:, 4 * P:], [[0, 48]], 0, 0)
+    i_16 = iota(T.i16[:], [[0, 8], [1, 16], [0, 4]], 0, 0)
 
-    def diag(c, before):
-        return [ts([c_id, c_stage] + before, T.stage[:, 512 * b + b:512 * (b + 1):4], T.ident[:], c, OP.mult) for b in range(4)]
+    c_z = run("fill", [], T.stq[:], 0.0)
+    c_q = ts([c_z, i_idx], T.stq[:, 3:515:4], T.idx[:], 0.0, OP.is_equal, 0.25, OP.mult)
+    c_m = run("act", [c_q], T.stm[:], T.stq[:], AF.Copy, scale=-2.0)
+    c_1 = run("act", [c_q], T.st1[:], T.stq[:], AF.Copy, scale=4.0)
+    u4 = [lin([lu], T.ub[:, t:512:4], T.idx[:], 0.0, T.tu[:, t:t + 1]) for t in range(4)]
 
-    def pack(name, d):
-        return quant(d, cols(name, 0, 512), T.stage[:])
+    def strips(c, d, strip):
+        return [quant([d], E[c][b], strip[:, 3 - b:515 - b]) for b in range(4)]
 
-    u4 = [run("act", [lu, c_z], T.ub[:, t:512:4], T.z128[:], AF.Identity, bias=T.tu[:, t:t + 1]) for t in range(4)]
-    d = diag(0.25, [])
-    v_l = ts([i_p], T.lint[:], T.pint[:], 15, OP.bitwise_and)
-    v_j = run("copy", [i_p], T.jc[:], T.pint[:])
-    v_cz = run("fill", [], T.cz[:], 0.0)
-    k_eq = pack("eq", d)
-    v_lf = run("copy", [v_l], T.lf[:], T.lint[:])
-    v_am = ts([i_am], T.am15[:], T.am[:], 15, OP.bitwise_and)
-    d = diag(1.0, [k_eq])
-    v_hf = run("tt", [v_lf, v_j], T.hf[:], T.jc[:], T.lf[:], OP.subtract)
-    v_z = [run("copy", [v_cz, v_lf], T.cz[:, 2:3], T.lf[:]),
-           run("copy", [v_cz, v_lf], T.cz[64:128, 3:4], T.lf[64:128, :])]
-    k_e1 = pack("e1", d)
-    v_h1 = ts([v_hf], T.h1[:], T.hf[:], 64.0, OP.add)
-    sh = {"A": [quant([ll], win("A", 0, 0, P), T.tl[:])], "H": [quant([lc], win("H", 0, 0, P), T.tc[:])]}
-    d = diag(-0.5, [k_e1])
-    v_z += [run("copy", [v_cz, v_hf], T.cz[:, 0:1], T.hf[:]),
-            run("copy", [v_cz, v_h1], T.cz[64:128, 1:2], T.h1[64:128, :])]
-    k_em = pack("em", d)
-    sh["B"] = [quant([lr], win("B", 0, 0, P), T.tr[:])]
-    v_e = [run("act", [c_z] + v_z, T.cet[:, t:512:4], T.z128[:], AF.Identity, bias=T.cz[:, t:t + 1]) for t in range(4)]
+    kE = {"eq": strips("eq", c_q, T.stq), "em": strips("em", c_m, T.stm)}
+    sh = {"A": [quant([ll], win("A", 0, 0, P), T.tl[:])]}
     k_u = quant(u4, U, T.ub[:])
+    sh["B"] = [quant([lr], win("B", 0, 0, P), T.tr[:])]
+    sh["H"] = [quant([lc], win("H", 0, 0, P), T.tc[:])]
+    kE["e1"] = strips("e1", c_1, T.st1)
+
+    hf, h1 = T.hf[:, 0:1], T.h1[:, 0:1]
+    a_hp = run("act", [i_s], T.junk[:], T.s16[:], AF.Identity, accum_out=T.hp[:])
+    a_n = lin([a_hp, i_p], T.nlf[:], T.hp[:], bias=T.npc[:])
+    a_hf = lin([a_hp], hf, T.hp[:], bias=-16.0)
+    a_h1 = lin([a_hp], h1, T.hp[:], bias=48.0)
+    a_lf = lin([a_n], T.lf[:], T.nlf[:], scale=-1.0)
+    a_th = [lin([a_n], T.th[:, 0:1], T.nlf[:], 1 / 16, (P + K) / 16), lin([a_n], T.th[:, 1:2], T.nlf[:], 1 / 16, (P + K - 1024) / 16)]
+    a_in = lin([a_n], T.ini[:, 0:1], T.nlf[:], 1 / up, P / up)
+    a_k = [lin([a_n, i_k], T.kq[:, h:2 * NE:2], T.k51[:], bias=T.nlf[:]) for h in range(2)]
+    a_b = [lin(a_th + [i_bm], T.below[:], T.bm[:], T.th[:, 0:1]), lin(a_th + [i_bm], T.above[:], T.bm[:], T.th[:, 1:2], 1024.0)]
+    a_e = [lin([i_idx, a_hf], T.cet[:, 0:512:4], T.idx[:], 0.0, hf),
+           lin([i_idx, a_lf], T.cet[:, 2:512:4], T.idx[:], 0.0, T.lf[:]),
+           lin([i_idx, a_h1], T.cet[64:128, 1:512:4], T.idx[64:128, :], 0.0, T.h1[64:128, 0:1]),
+           lin([i_idx, a_lf], T.cet[64:128, 3:512:4], T.idx[64:128, :], 0.0, T.lf[64:128, :]),
+           lin([c_q], T.cet[0:64, 1:512:2], T.stq[0:64, 0:256], 0.0)]
+    a_s = run("act", [i_17, a_n], T.m1[:], T.i17[:], AF.Sign, bias=T.nlf[:])
+    a_1 = run("act", [a_s], T.m2[:], T.m1[:], AF.Abs)
+    a_r = run("act", [a_s], T.es[:], T.m1[:], AF.Relu)
+    a_1 = lin([a_1], T.m2[:], T.m2[:], -up, up)
 
     free = {(k, b): [] for b in range(4) for k in "ZH"}
+    tH, tZ = {}, {}
 
-    def decode_h(t):
-        return [mm(sh["H"] + free["H", b] + [k_e1], psH[b][:, 0:P], E["e1"][b], win("H", t, 0, P)) for b in range(4)]
+    def decode(t, steps):
+        for k, b in steps.split():
+            b = int(b)
+            if k == "h":
+                tH[b] = mm(sh["H"] + free["H", b] + [kE["e1"][b]], psH[b][:, 0:P], E["e1"][b], win("H", t, 0, P))
+            elif k == "A":
+                mm(sh["A"] + free["Z", b] + [kE["eq"][b]], psZ[b][:, 0:P], E["eq"][b], win("A", t, 0, P), True, False)
+            elif k == "B":
+                mm(sh["B"], psZ[b][:, 0:P], E["eq"][b], win("B", t, 0, P), False, False)
+            else:
+                tZ[b] = mm(sh["H"] + [kE["em"][b]], psZ[b][:, 0:P], E["em"][b], win("H", t, 0, P), False, True)
 
-    def decode_a(t):
-        for b in range(4):
-            mm(sh["A"] + free["Z", b] + [k_eq], psZ[b][:, 0:P], E["eq"][b], win("A", t, 0, P), True, False)
-
-    def decode_bh(t):
-        z = []
-        for b in range(4):
-            mm(sh["B"], psZ[b][:, 0:P], E["eq"][b], win("B", t, 0, P), False, False)
-            z.append(mm([k_em], psZ[b][:, 0:P], E["em"][b], win("H", t, 0, P), False, True))
-        return z
-
-    decode_a(0)
-    tH = decode_h(0)
-    tZ = decode_bh(0)
+    decode(0, FIRST)
 
     def send(deps, src, to_right, to_left, t):
         wait("g", deps)
@@ -178,124 +198,145 @@ def rank_program(g, core, T, topo):
 
     got = {"A": 2 * len(topo.engines(left, core)[0::2]), "B": 2 * len(topo.engines(right, core)[1::2])}
     chtok = []
+    k = {}
 
     for t in range(R):
         last = t == R - 1
-        tx, td = {}, {}
-        for step in STEPS.split():
-            b = int(step[1])
-            x = XS[t + 1][:, row[b]]
-            if step[0] == "x":
-                tx[b] = run("tt", [tZ[b], lx], x, psZ[b][:, 0:P], XS[t][:, row[b]], OP.add)
+        for s in DRIFT.split():
+            c, e = (0, L) if s[-1] == "L" else (L, P)
+            if s[0] == "q":
+                if t == 0 and c:
+                    k["ce"] = quant(a_e, CE, T.cet[:])
+                k[s] = quant([k["d%d%s" % (b, s[-1])] for b in range(4)] + ([i_zd] if c else []), cols("dq", c, c + L),
+                             T.dtile[:, 4 * c:4 * c + 4 * L])
+                continue
+            b = int(s[1])
+            part = slice(4 * c + b, 4 * e, 4)
+            if s[0] == "x":
+                k[s] = run("tt", [tZ[b], lx], XS[t + 1][:, part], psZ[b][:, c:e], XS[t][:, part], OP.add)
             else:
-                td[b] = run("tt", [tx[b], tH[b]], T.dtile[:, row[b]], x, psH[b][:, 0:P], OP.subtract)
-        tq = quant(list(td.values()), DQ, T.dtile[:])
+                k[s] = run("tt", [k["x" + s[1:]], tH[b]], T.dtile[:, part], XS[t + 1][:, part], psH[b][:, c:e], OP.subtract)
+        q0, q1 = k["qL"], k["qR"]
+        mr0 = mm([q0, k_u, k["x0R"]], psZ[0][:, 0:L], U, cols("dq", 0, L))
+        mc0 = mm([q0, k["x1R"]], psZ[1][:, 0:128], cols("dq", 0, L), U)
+        for b in range(2):
+            mm([k["x%dR" % (2 + b)]], psS[b][:, 0:P], E["e1"][b], win("H", t, 0, P), True, False)
+        mc1 = mm([q1], psH[1][:, 0:128], cols("dq", 64, P), U)
+        mr1 = mm([q1], psH[0][:, 0:L], U, cols("dq", L, 2 * L))
+        mS = []
         for b in range(4):
-            mm([tx[b]], psZ[b][:, 0:P], E["e1"][b], win("H", t, 0, P), True, False)
-        mr = mm([tq, k_u], psH[0][:, 0:P], U, DQ)
-        mc0 = mm([tq], psH[1][:, 0:128], cols("dq", 0, 128), U)
-        mc1 = mm([tq], psH[2][:, 0:128], cols("dq", 64, 192), U)
-        mS = [mm([tq], psZ[b][:, 0:P], E["e1"][b], DQ, False, True) for b in range(4)]
-
-        def minus(m, bank, h):
-            return run("red", [m], T.nsc[:, h:h + 1], bank[:, 0:2], AxisListType.X, OP.max, negate=True,
-                       apply_absolute_value=True)
-
+            if b >= 2:
+                mm([q1], psS[b][:, 0:P], E["e1"][b], win("H", t, 0, P), True, False)
+            mS.append(mm([q1], psS[b][:, 0:P], E["e1"][b], DQ, False, True))
+        ar0 = run("act", [mr0], T.sab[:, 0:L], psZ[0][:, 0:L], AF.Abs)
+        ac0 = run("act", [mc0], T.aj[:, 0:1], psZ[1][:, 0:1], AF.Abs)
+        ac1 = run("act", [mc1], T.aj[:, 1:2], psH[1][:, 0:1], AF.Abs)
+        ar1 = run("act", [mr1], T.sab[:, L:P], psH[0][:, 0:P - L], AF.Abs)
+        aS = [run("act", [mS[b]], T.stile[:, b:4 * P:4], psS[b][:, 0:P], AF.Copy) for b in range(4)]
         if t == 0:
-            v_f = [run("fill", [], T.g0[:, P:P + 16], float(P)), run("fill", [], T.g1[:, P:P + 16], float(P)),
-                   run("fill", [], T.ot[:, 384:512], 0.0)]
-            v_k = [run("copy", [i_k], T.k192[:, h:192:2], T.k96[:]) for h in range(2)]
-            k_ce = [quant(v_e, CE, T.cet[:])]
-        n0, n1 = T.nsc[:, 0:1], T.nsc[:, 1:2]
-        aA = [run("act", [mr], T.sab[:, c:e], psH[0][:, c:e], AF.Abs) for c, e in ((0, 128), (128, P))]
-        aS = [run("act", [mS[b]], T.stile[:, row[b]], psZ[b][:, 0:P], AF.Copy) for b in range(4)]
-        if last:
-            axo = run("act", list(tx.values()), T.xout[:], XS[R][:], AF.Copy)
-            store("s", [axo], T.xe[:], T.xout[:])
-        vc0 = minus(mc0, psH[1], 0)
-        vc1 = minus(mc1, psH[2], 1)
-        vd0 = ts([aA[0], vc0], T.df[:, 0:128], T.sab[:, 0:128], n0, OP.add)
-        vi1 = ts([aA[0], vc1], T.g1[:, 0:128], T.sab[:, 0:128], n1, OP.add, 0.0, OP.is_ge)
-        vd1 = ts([aA[1], vc1], T.df[:, 128:P], T.sab[:, 128:P], n1, OP.add)
-        vi0 = ts([aA[1], vc0], T.g0[:, 128:P], T.sab[:, 128:P], n0, OP.add, 0.0, OP.is_gt)
-        vg0 = run("tt", [vd0, i_t0], T.g0[:, 0:128], T.df[:, 0:128], T.thr[:, 0:128], OP.is_gt)
-        vg1 = run("tt", [vd1, i_t1], T.g1[:, 128:P], T.df[:, 128:P], T.thr[:, 128:P], OP.is_gt)
-        if t == 0:
-            v_b = [ts([i_r, v_hf], T.bm[:, 0:8], T.row16[:, 0:8], T.hf[:], OP.is_equal),
-                   ts([i_r, v_h1], T.bm[:, 8:12], T.row16[:, 8:12], T.h1[:], OP.is_equal)]
-        vr0 = run("red", [vg0, vi0] + v_f, T.rr[:, 0:1], T.g0[:, 0:P + 1], AxisListType.X, OP.add)
-        vr1 = run("red", [vg1, vi1] + v_f, T.rr[:, 1:2], T.g1[:, 0:P + 1], AxisListType.X, OP.add)
-        if t == 0:
-            v_b = [ts(v_b, T.below[:], T.bm[:], float(P + K), OP.mult),
-                   ts(v_b, T.above[:], T.bm[:], P + K - 1000000.0, OP.mult, 1000000.0, OP.add),
-                   run("fill", [], T.xt[:], 0.0)]
-        r0, r1 = T.rr[:, 0:1], T.rr[:, 1:2]
-        vo0 = ts([vr0] + v_k, T.ot[:, 0:384:2], T.k192[:], r0, OP.is_equal)
-        vx = [ts([vr0] + v_b, T.xf[:, 0:8], T.below[:, 0:8], r0, OP.is_gt, r0, OP.mult)]
-        vo1 = ts([vr1] + v_k, T.ot[:, 1:384:2], T.k192[:], r1, OP.is_equal)
-        vx.append(ts([vr1] + v_b, T.xf[:, 8:12], T.below[:, 8:12], r1, OP.is_gt, r1, OP.mult))
-        vj = [ts([vr0] + v_b, T.xt[:, e:32:4], T.above[:, 0:8], r0, OP.is_le, c[:], OP.mult) for e, c in ((1, T.hf), (3, T.lf))]
-        vqo = quant([vo0, vo1], OQ, T.ot[:])
-        me = mm([vqo] + k_ce, psH[3][:, 0:128], CE, OQ)
-        S, eo = cols("sq%d" % t, 0, P), T["eo%d" % t]
+            wait("s", [q1])
+            lw = load("s", "lw", T.tw[:], T.w[:])
+        a0, a1 = T.aj[:, 0:1], T.aj[:, 1:2]
+        s0, s1 = T.sab[:, 0:L], T.sab[:, L:P]
+        ini = T.ini[:, 0:1]
+        r0, r1 = T.acc[:, N0 - 1:N0], T.acc[:, N1 - 1:N1]
+        X = [T.stile[:, 4 * P + e:4 * P + 48:4] for e in range(2)]
         big = 1.5 * 2.0 ** 27
-        vh = ts(vx, T.xt[:, 0:48:4], T.xf[:], big, OP.add, big, OP.subtract)
-        vj += [ts([vr1], T.xt[:, 32 + e:48:4], T.above[:, 8:12], r1, OP.is_le, c[:], OP.mult) for e, c in ((1, T.h1), (3, T.lf))]
-        vl = run("tt", [vh], T.xt[:, 2:48:4], T.xf[:], T.xt[:, 0:48:4], OP.subtract)
-        vqs = quant(aS, S, T.stile[:])
-        H, X, msg = win("H", t, P, P + K), win("H", t, P + K, P + K + 128), win("H", t, P, SND)
-        ve = run("tr", [me], T.etr[:], psH[3][:, 0:96])
-        vqx = quant([vl, vh] + vj, X, T.xt[:])
-        veo = run("copy", [ve], eo[:, 0:3], T.etr[:, 0:96:32])
-        vp = run("copy", [veo, vqs], H[0].bitcast(dt.uint32), S[0].bitcast(dt.uint32).indirect(eo[:, 0:3]))
-        ap = run("act", [veo, vqs], H[1], S[1].indirect(eo[:, 0:3]), AF.Copy)
+        S, eo = cols("sq%d" % t, 0, P + 12), T.eo
+        H, msg = win("H", t, P, P + 64), win("H", t, P, SND)
+
+        def scan(deps, a, b, first):
+            return run("scan", deps, T.acc[:, a:b], T.mul[:, a:b], T.cmp[:, a:b], first, OP.mult, OP.add)
+
+        def onehots():
+            q = quant([k["o0"], k["o1"], i_zo], OQ, T.ot[:])
+            k["me"] = mm([q, k["ce"], ar0], psZ[0][:, 0:128], CE, OQ)
+            return q
+
+        def chosen():
+            deps = [k["eo"], k["qs"], k["e3"]]
+            k["ap"] = run("act", deps, H[1], S[1].indirect(eo[:]), AF.Copy)
+            return run("copy", deps, H[0].bitcast(dt.uint32), S[0].bitcast(dt.uint32).indirect(eo[:]))
+
+        calls = {
+            "eq0": lambda: ts([ar0, ac0], T.cmp[:, 0:L], s0, a0, OP.is_equal, 1 / up, OP.mult),
+            "gt0": lambda: ts([ar0, ac0], T.cmp[:, L:2 * L], s0, a0, OP.is_gt),
+            "gR0": lambda: ts([ar1, ac0], T.cmp[:, 2 * L:N0], s1, a0, OP.is_gt),
+            "ge1": lambda: ts([ar0, ac1], T.cmp[:, N0 + 64:N0 + 64 + L], s0, a1, OP.is_ge),
+            "eq1": lambda: ts([ar1, ac1], T.cmp[:, N0:N0 + 64], s1, a1, OP.is_equal, 1 / up, OP.mult),
+            "gt1": lambda: ts([ar1, ac1], T.cmp[:, N0 + 64 + L:N1], s1, a1, OP.is_gt),
+            "sL0": lambda: scan([k["eq0"], k["gt0"], a_in] + i_m, 0, 2 * L, ini),
+            "sR0": lambda: scan([k["sL0"], k["gR0"]], 2 * L, N0, T.acc[:, 2 * L - 1:2 * L]),
+            "s1": lambda: scan([k["ge1"], k["eq1"], k["gt1"]], N0, N1, ini),
+            "o0": lambda: ts([k["sR0"]] + a_k, T.ot[:, 0:4 * NE:2], T.kq[:], r0, OP.is_equal),
+            "o1": lambda: ts([k["s1"]], T.ot[:, 1:4 * NE:2], T.kq[:], r1, OP.is_equal),
+            "a0": lambda: ts([k["sR0"]] + a_b, T.xf[:, 0:8], T.below[:], r0, OP.is_gt, r0, OP.mult),
+            "a1": lambda: ts([k["s1"]], T.xf[:, 8:12], T.below[:, 4:8], r1, OP.is_gt, r1, OP.mult),
+            "b0": lambda: ts([k["sR0"], i_zx, a_hf] + a_b, T.stile[:, 4 * P + 2:4 * P + 32:4], T.above[:], r0, OP.is_le, hf, OP.mult),
+            "b1": lambda: ts([k["s1"], a_h1], T.stile[:, 4 * P + 34:4 * P + 48:4], T.above[:, 4:8], r1, OP.is_le, h1, OP.mult),
+            "hi": lambda: ts([k["a0"], k["a1"], i_zx], X[0], T.xf[:], big, OP.add, big, OP.subtract),
+            "lo": lambda: run("tt", [k["hi"]], X[1], T.xf[:], X[0], OP.subtract),
+            "qo": onehots,
+            "es": lambda: run("scan", [k["me"], k["mf"]], T.es[:], psZ[0][:, 0:NE], T.me[:], 0.0, OP.add, OP.mult),
+            "qs": lambda: quant(aS + [k["lo"], k["b0"], k["b1"]], S, T.stile[:]),
+            "eo": lambda: ts([k["es"]], eo[:, 0:3], T.es[:, 16:NE:17], 1 / up, OP.mult),
+            "pick": chosen,
+        }
+        for s in RANKS.split() + LISTS.split():
+            k[s] = calls[s]()
+            if t == 0 and s == "gt0":
+                k["e3"] = ts([a_lf], T.eo[:, 3:4], T.lf[:], 11.0, OP.min, float(P), OP.add)
+                k["mf"] = run("tt", [a_1, a_r], T.me[:], T.m2[:], T.es[:], OP.add)
+        vp, ap, ve = k["pick"], k["ap"], k["es"]
         da, db = win("A", t, P, SND), win("B", t, P, SND)
-        send([vp, vqx], msg[0].bitcast(dt.uint8), da[0].bitcast(dt.uint8), db[0].bitcast(dt.uint8), t)
-        send([ap, vqx], msg[1], da[1], db[1], t)
-        ach = [run("act", [ve], T.chs[0:1, K * t + 16 * m:K * t + 16 * m + 16], psH[3][0:1, 32 * m:32 * m + 16], AF.Copy)
+        send([vp], msg[0].bitcast(dt.uint8), da[0].bitcast(dt.uint8), db[0].bitcast(dt.uint8), t)
+        send([ap], msg[1], da[1], db[1], t)
+        ach = [run("act", [ve], T.chs[0:1, K * t + 16 * m:K * t + 16 * m + 16], psZ[0][0:1, 17 * m + 1:17 * m + 17], AF.Copy)
                for m in range(3)]
         chtok.append(ach[-1])
         if t == 0:
-            v_c = [ts([v_am], T.cst[:, h:512:4], T.am15[:], 0.0, OP.is_equal) for h in range(4)]
-            k_cs = quant(v_c, CS, T.cst[:])
+            v_c = ts([i_16, a_lf], T.cst[:], T.i16[:], T.lf[:], OP.is_equal)
+            k_cs = quant([v_c], CS, T.cst[:])
+        if last:
+            store("s", chtok, T.ch[:], T.chs[0:1, :])
+            axo = run("act", [q1], T.xout[:], XS[R][:], AF.Copy)
+            store("s", [axo], T.xe[:], T.xout[:])
 
-        def places(k, deps, bank, tile, c):
-            m = mm(deps + [k_cs], bank[:, 0:128], CS, tile)
-            return lambda: run("copy", [m], T["so%s%d" % (k, t)][:], bank[:, c:c + 12])
+        def places(c, deps, bank):
+            m = mm(deps + [k_cs], bank[:, 0:128], CS, win(c, t, SND - 128, SND))
+            return lambda: ts([m], T["so%s%d" % (c, t)][:], bank[:, 116:128], T.lf[:], OP.add)
 
-        def pick(k, deps):
-            so, d, w = T["so%s%d" % (k, t)], win(k, t + 1, 0, P), cols("w%s%d" % (k, t), 0, SND)
+        def pick(c, deps):
+            so, d, w = T["so%s%d" % (c, t)], win(c, t + 1, 0, P), cols("w%s%d" % (c, t), 0, SND)
             return [run("copy", deps, d[0].bitcast(dt.uint32), w[0].bitcast(dt.uint32).indirect(so[:])),
                     run("act", deps, d[1], w[1].indirect(so[:]), AF.Copy)]
 
-        vsh = places("H", [vqx, aS[0]], psZ[0], X, 0)()
-        sh["H"] = pick("H", [vsh, vp, ap])
-        for b, d in enumerate((aA, [vc0], [vc1], ach + [ve])):
-            free["H", b] = d
+        vsh = places("H", [vp, ap, ac0], psZ[1])()
+        sh["H"] = pick("H", [vsh])
+        for b, d in enumerate((ar1, ac1, aS[2], aS[3])):
+            free["H", b] = [d]
         if not last:
-            tH = decode_h(t + 1)
+            decode(t + 1, "h0 h1 h2 h3")
         else:
             k_w = quant([lw], cols("wq", 0, 128), T.tw[:])
-            store("s", chtok, T.ch[:], T.chs[0:1, :])
-            store("s", sh["H"], T.oc[:, 4 * P:8 * P], T.fin[:, P:2 * P].bitcast(dt.uint8))
+            store("s", sh["H"][:1], T.oc[:, 4 * P:8 * P], T.fin[:, P:2 * P].bitcast(dt.uint8))
         ra, rb = ("rA%d" % t, got["A"]), ("rB%d" % t, got["B"])
-        la = places("A", [ra, aS[2]], psZ[2], win("A", t, SND - 128, SND), 116)
-        lb = places("B", [rb, aS[3]], psZ[3], win("B", t, SND - 128, SND), 116)
+        la = places("A", [ra, aS[0]], psZ[2])
+        lb = places("B", [rb, aS[1]], psZ[3])
         vsa = la()
-        sh["A"] = pick("A", [vsa, ra])
         vsb = lb()
+        sh["A"] = pick("A", [vsa, ra])
         sh["B"] = pick("B", [vsb, rb])
-        for b, d in enumerate((vsh, aS[1], vsa, vsb)):
-            free["Z", b] = [d]
+        for b, d in enumerate((ach + [ve], [vsh], [vsa], [vsb])):
+            free["Z", b] = d
         if not last:
-            decode_a(t + 1)
-            tZ = decode_bh(t + 1)
+            decode(t + 1, LATER)
 
     my = mm(sh["A"] + free["Z", 0] + [k_w], psZ[0][:, 0:P], cols("wq", 0, 128), win("A", R, 0, P))
     vy = run("copy", [my], T.yout[:], psZ[0][:, 0:P])
-    store("s", sh["A"], T.oc[:, 0:4 * P], T.fin[:, 0:P].bitcast(dt.uint8))
-    store("s", sh["B"], T.oc[:, 8 * P:12 * P], T.fin[:, 2 * P:3 * P].bitcast(dt.uint8))
-    for k in range(4):
-        store("a" if k % 2 else "s", sh["A"] + sh["B"] + sh["H"], T.osc[4 * k:4 * k + 4, :], T.fin_s[32 * k:32 * k + 4, :])
-    store("a", [vy], T.y[:], T.yout[:])
+    store("s", sh["A"][:1], T.oc[:, 0:4 * P], T.fin[:, 0:P].bitcast(dt.uint8))
+    store("s", sh["B"][:1], T.oc[:, 8 * P:12 * P], T.fin[:, 2 * P:3 * P].bitcast(dt.uint8))
+    for j in range(4):
+        store("a" if j else "s", sh["A"] + sh["B"] + sh["H"], T.osc[4 * j:4 * j + 4, :], T.fin_s[32 * j:32 * j + 4, :])
+    store("s", [vy], T.y[:], T.yout[:])
     wait("g", [("s" + q, c) for q, c in cnt.items()] + list(total.items()))

@@ -4,19 +4,20 @@ from concourse.mybir import dt, AluOpType as OP, ActivationFunctionType as AF
 P, K, R = 192, 48, 3
 L = 128
 BF, F32, U16, FP8, U8 = "bfloat16", "float32", "uint16", "float8_e4m3fn_x4", "uint8"
-SND = P + K + 12
+W0 = 32
 N0, N1 = L + P, L + P + P + P - L
 NE = 51
-DRIFT = "x0L x0R x1L d0L x1R x2L d1L x3L d2L d3L x2R x3R qL d0R d1R d2R d3R qR"
+DRIFT = ("x0L x0R x1L d0L x1R x2L d1L x3L d2L d3L x2R x3R qL d0R d1R d2R d3R qR",
+         "x0L x1L x2L T0 T1 T2 d0L x3L d1L d2L d3L x0R x1R qL x3R x2R d0R d1R d3R d2R qR")
 RANKS = "eq0 gt0 sL0 ge1 gR0 eq1 gt1 sR0 s1"
-LISTS = "o0 a0 o1 a1 b0 qo hi b1 lo es qs eo pick"
+LISTS = "a0 o0 a1 o1 b0 hi qo lo b1 qx es qs eo pick"
 FIRST = "A0 A1 A2 A3 B0 B1 B2 B3 H0 H1 h0 H2 h1 H3 h2 h3"
-LATER = "A0 A1 A2 B0 H0 B1 H1 B2 H2 A3 B3 H3"
+LATER = "A0L A1L A2L B0L H0L B1L H1L B2L H2L A3 B3 H3"
 
 SCRATCH = {}
 SCRATCH.update({n: ("sbuf", [128, w], BF) for n, w in dict(
     x0=768, x1=768, x2=768, x3=768, tl=768, tc=768, tr=768, tu=4, tw=512, ub=512, idx=128, stq=516, stm=516, st1=516,
-    cet=512, cst=512, i16=512, k51=NE, kq=2 * NE, dtile=1024, stile=4 * (P + 12), cmp=N1, mul=N1, acc=N1, ot=512,
+    cet=512, cst=512, i16=512, k51=NE, kq=2 * NE, dtile=1024, stile=4 * P, xt=512, cmp=N1, mul=N1, acc=N1, ot=512,
     ini=2, hf=2, h1=2).items()})
 SCRATCH.update({n: ("sbuf", [128, w], F32) for n, w in dict(
     npc=1, c16=8, s16=8, junk=8, bm=8, hp=1, lf=1, nlf=1, th=2, below=8, above=8, sab=192, aj=2, xf=12,
@@ -24,8 +25,9 @@ SCRATCH.update({n: ("sbuf", [128, w], F32) for n, w in dict(
 SCRATCH["eo"] = ("sbuf", [128, 4], U16)
 _Q = dict(uq=128, wq=128, e1=512, eq=512, em=512, ce=128, cs=128, dq=256, oq=128, fin=3 * P)
 for _t in range(R):
-    _Q.update({"wA%d" % _t: SND, "wB%d" % _t: SND, "wH%d" % _t: P + 64, "sq%d" % _t: P + 12})
+    _Q.update({"sq%d" % _t: P, "xq%d" % _t: 128})
     for _n in "AHB":
+        _Q["w%s%d" % (_n, _t)] = W0 + P + K
         SCRATCH["so%s%d" % (_n, _t)] = ("sbuf", [128, 12], U16)
 for _n, _w in _Q.items():
     SCRATCH[_n] = ("sbuf", [128, _w], FP8)
@@ -35,7 +37,7 @@ for _b in range(4):
     SCRATCH["psH%d" % _b] = ("psum", [128, 512], F32)
 
 SEMAPHORES = (["sv", "sa", "st", "sg", "left", "lc", "ll", "lr", "lx", "lu", "lw", "out"]
-              + ["rA%d" % t for t in range(R)] + ["rB%d" % t for t in range(R)])
+              + [_s + str(_t) for _t in range(R) for _s in ("rA", "rB", "pA", "pB")])
 
 
 def rank_program(g, core, T, topo):
@@ -94,7 +96,7 @@ def rank_program(g, core, T, topo):
 
     def win(k, t, a, b):
         o = P * "AHB".index(k)
-        return cols("fin", o + a, o + b) if t == R else cols("w%s%d" % (k, t), a, b)
+        return cols("fin", o + a, o + b) if t == R else cols("w%s%d" % (k, t), W0 + a, W0 + b)
 
     def mm(deps, out, l, r, start=True, stop=True):
         return run("mm", deps, out, l[0], l[1], r[0], r[1], start, stop)
@@ -126,13 +128,12 @@ def rank_program(g, core, T, topo):
     i_17 = iota(T.i17[:], [[0, 3], [1, 17]], -1, 0)
     i_zd = iota(T.dtile[:, 4 * P:], [[0, 1024 - 4 * P]], 0, 0)
     i_m = iota(T.mul[:], [[0, N1]], 1, 0)
-    i_zo = iota(T.ot[:, 4 * NE:], [[0, 512 - 4 * NE]], 0, 0)
+    i_16 = iota(T.i16[:], [[0, 8], [1, 16], [0, 4]], 0, 0)
     i_m = [run("select", [i_m], T.mul[:, 0:L], T.mul[:, 0:L], [[1, L]], OP.not_equal, up, 0, -1),
            run("select", [i_m], T.mul[:, N0:N0 + 64], T.mul[:, N0:N0 + 64], [[1, 64]], OP.not_equal, up, 64, -1)]
-    i_zx = iota(T.stile[:, 4 * P:], [[0, 48]], 0, 0)
-    i_16 = iota(T.i16[:], [[0, 8], [1, 16], [0, 4]], 0, 0)
 
     c_z = run("fill", [], T.stq[:], 0.0)
+    i_zo = run("fill", [], T.ot[:, 4 * NE:], 0.0)
     c_q = ts([c_z, i_idx], T.stq[:, 3:515:4], T.idx[:], 0.0, OP.is_equal, 0.25, OP.mult)
     c_m = run("act", [c_q], T.stm[:], T.stq[:], AF.Copy, scale=-2.0)
     c_1 = run("act", [c_q], T.st1[:], T.stq[:], AF.Copy, scale=4.0)
@@ -164,58 +165,70 @@ def rank_program(g, core, T, topo):
            lin([i_idx, a_lf], T.cet[64:128, 3:512:4], T.idx[64:128, :], 0.0, T.lf[64:128, :]),
            lin([c_q], T.cet[0:64, 1:512:2], T.stq[0:64, 0:256], 0.0)]
     a_s = run("act", [i_17, a_n], T.m1[:], T.i17[:], AF.Sign, bias=T.nlf[:])
+    i_zx = lin([c_q], T.xt[:], T.stq[:, 0:512], 0.0)
     a_1 = run("act", [a_s], T.m2[:], T.m1[:], AF.Abs)
     a_r = run("act", [a_s], T.es[:], T.m1[:], AF.Relu)
     a_1 = lin([a_1], T.m2[:], T.m2[:], -up, up)
 
     free = {(k, b): [] for b in range(4) for k in "ZH"}
-    tH, tZ = {}, {}
+    tH, tZ, k = {}, {}, {}
 
     def decode(t, steps):
-        for k, b in steps.split():
-            b = int(b)
-            if k == "h":
+        for w in steps.split():
+            c, b, part = w[0], int(w[1]), w[2:]
+            a, e = {"": (0, P), "L": (0, L), "R": (P - L, P)}[part]
+            if c == "h":
                 tH[b] = mm(sh["H"] + free["H", b] + [kE["e1"][b]], psH[b][:, 0:P], E["e1"][b], win("H", t, 0, P))
-            elif k == "A":
-                mm(sh["A"] + free["Z", b] + [kE["eq"][b]], psZ[b][:, 0:P], E["eq"][b], win("A", t, 0, P), True, False)
-            elif k == "B":
-                mm(sh["B"], psZ[b][:, 0:P], E["eq"][b], win("B", t, 0, P), False, False)
-            else:
-                tZ[b] = mm(sh["H"] + [kE["em"][b]], psZ[b][:, 0:P], E["em"][b], win("H", t, 0, P), False, True)
+                continue
+            tile = "em" if c == "H" else "eq"
+            deps = [kE[tile][b]] + sh[c if c == "H" else c + part]
+            if c == "A":
+                deps = deps + ([k["x%dL" % b]] if part == "R" else free["Z", b])
+            m = mm(deps, psZ[b][:, 0:e - a], E[tile][b], win(c, t, a, e), c == "A", c == "H")
+            if c == "H":
+                for p, c0, c1 in (("L", 0, L), ("R", L, P)):
+                    if part in ("", p):
+                        tZ[b, p] = (m, psZ[b][:, c0 - a:c1 - a])
 
     decode(0, FIRST)
 
-    def send(deps, src, to_right, to_left, t):
-        wait("g", deps)
-        tr = []
-        for who, dst, sem, odd in ((right, to_right, "rA%d" % t, 0), (left, to_left, "rB%d" % t, 1)):
-            rid, pid, _ = topo.addr(who)
-            eng = topo.engines(core, who)[odd::2]
-            tr.append(RemoteDMATransfer(dst_ids=[DstId(rid=rid, pnc=pid)], dma_engine_mask=sum(1 << e for e in eng),
-                                        remote_sem=T.sem[sem], src=src, dst=dst))
-            total["left"] += len(eng)
-        g.remote_dma_fused(tr, local_sem=T.sem.left)
+    def send(deps, src, what, t, a, b):
+        for kind in range(2):
+            wait("g", [deps[kind]])
+            tr = []
+            for who, c, side in ((right, "A", 0), (left, "B", 1)):
+                rid, pid, _ = topo.addr(who)
+                eng = topo.engines(core, who)[side::2]
+                s, d = src[kind], win(c, t, a, b)[kind]
+                if kind == 0:
+                    s, d = s.bitcast(dt.uint8), d.bitcast(dt.uint8)
+                tr.append(RemoteDMATransfer(dst_ids=[DstId(rid=rid, pnc=pid)], dma_engine_mask=sum(1 << e for e in eng),
+                                            remote_sem=T.sem[what + c + str(t)], src=s, dst=d))
+                total["left"] += len(eng)
+            g.remote_dma_fused(tr, local_sem=T.sem.left)
 
     got = {"A": 2 * len(topo.engines(left, core)[0::2]), "B": 2 * len(topo.engines(right, core)[1::2])}
     chtok = []
-    k = {}
 
     for t in range(R):
         last = t == R - 1
-        for s in DRIFT.split():
+        for s in DRIFT[min(t, 1)].split():
             c, e = (0, L) if s[-1] == "L" else (L, P)
-            if s[0] == "q":
+            if s[0] == "T":
+                decode(t, "A%sR B%sR H%sR" % (s[1], s[1], s[1]))
+            elif s[0] == "q":
                 if t == 0 and c:
                     k["ce"] = quant(a_e, CE, T.cet[:])
                 k[s] = quant([k["d%d%s" % (b, s[-1])] for b in range(4)] + ([i_zd] if c else []), cols("dq", c, c + L),
                              T.dtile[:, 4 * c:4 * c + 4 * L])
-                continue
-            b = int(s[1])
-            part = slice(4 * c + b, 4 * e, 4)
-            if s[0] == "x":
-                k[s] = run("tt", [tZ[b], lx], XS[t + 1][:, part], psZ[b][:, c:e], XS[t][:, part], OP.add)
             else:
-                k[s] = run("tt", [k["x" + s[1:]], tH[b]], T.dtile[:, part], XS[t + 1][:, part], psH[b][:, c:e], OP.subtract)
+                b = int(s[1])
+                part = slice(4 * c + b, 4 * e, 4)
+                if s[0] == "x":
+                    m, z = tZ[b, s[-1]]
+                    k[s] = run("tt", [m, lx], XS[t + 1][:, part], z, XS[t][:, part], OP.add)
+                else:
+                    k[s] = run("tt", [k["x" + s[1:]], tH[b]], T.dtile[:, part], XS[t + 1][:, part], psH[b][:, c:e], OP.subtract)
         q0, q1 = k["qL"], k["qR"]
         mr0 = mm([q0, k_u, k["x0R"]], psZ[0][:, 0:L], U, cols("dq", 0, L))
         mc0 = mm([q0, k["x1R"]], psZ[1][:, 0:128], cols("dq", 0, L), U)
@@ -234,16 +247,14 @@ def rank_program(g, core, T, topo):
         ar1 = run("act", [mr1], T.sab[:, L:P], psH[0][:, 0:P - L], AF.Abs)
         aS = [run("act", [mS[b]], T.stile[:, b:4 * P:4], psS[b][:, 0:P], AF.Copy) for b in range(4)]
         if t == 0:
-            wait("s", [q1])
+            wait("s", [q0])
             lw = load("s", "lw", T.tw[:], T.w[:])
         a0, a1 = T.aj[:, 0:1], T.aj[:, 1:2]
         s0, s1 = T.sab[:, 0:L], T.sab[:, L:P]
         ini = T.ini[:, 0:1]
         r0, r1 = T.acc[:, N0 - 1:N0], T.acc[:, N1 - 1:N1]
-        X = [T.stile[:, 4 * P + e:4 * P + 48:4] for e in range(2)]
         big = 1.5 * 2.0 ** 27
-        S, eo = cols("sq%d" % t, 0, P + 12), T.eo
-        H, msg = win("H", t, P, P + 64), win("H", t, P, SND)
+        S, XQ, eo, H = cols("sq%d" % t, 0, P), cols("xq%d" % t, 0, 128), T.eo[:, 0:3], win("H", t, P, P + K)
 
         def scan(deps, a, b, first):
             return run("scan", deps, T.acc[:, a:b], T.mul[:, a:b], T.cmp[:, a:b], first, OP.mult, OP.add)
@@ -253,10 +264,15 @@ def rank_program(g, core, T, topo):
             k["me"] = mm([q, k["ce"], ar0], psZ[0][:, 0:128], CE, OQ)
             return q
 
+        def lists():
+            q = quant([k["lo"], k["b0"], k["b1"]], XQ, T.xt[:])
+            send([q, q], cols("xq%d" % t, 0, 12), "p", t, -12, 0)
+            return q
+
         def chosen():
-            deps = [k["eo"], k["qs"], k["e3"]]
-            k["ap"] = run("act", deps, H[1], S[1].indirect(eo[:]), AF.Copy)
-            return run("copy", deps, H[0].bitcast(dt.uint32), S[0].bitcast(dt.uint32).indirect(eo[:]))
+            deps = [k["eo"], k["qs"]]
+            k["ap"] = run("act", deps, H[1], S[1].indirect(eo), AF.Copy)
+            return run("copy", deps, H[0].bitcast(dt.uint32), S[0].bitcast(dt.uint32).indirect(eo))
 
         calls = {
             "eq0": lambda: ts([ar0, ac0], T.cmp[:, 0:L], s0, a0, OP.is_equal, 1 / up, OP.mult),
@@ -265,32 +281,30 @@ def rank_program(g, core, T, topo):
             "ge1": lambda: ts([ar0, ac1], T.cmp[:, N0 + 64:N0 + 64 + L], s0, a1, OP.is_ge),
             "eq1": lambda: ts([ar1, ac1], T.cmp[:, N0:N0 + 64], s1, a1, OP.is_equal, 1 / up, OP.mult),
             "gt1": lambda: ts([ar1, ac1], T.cmp[:, N0 + 64 + L:N1], s1, a1, OP.is_gt),
-            "sL0": lambda: scan([k["eq0"], k["gt0"], a_in] + i_m, 0, 2 * L, ini),
-            "sR0": lambda: scan([k["sL0"], k["gR0"]], 2 * L, N0, T.acc[:, 2 * L - 1:2 * L]),
+            "sL0": lambda: scan([k["eq0"], a_in] + i_m, 0, L, ini),
+            "sR0": lambda: scan([k["sL0"], k["gt0"], k["gR0"]], L, N0, T.acc[:, L - 1:L]),
             "s1": lambda: scan([k["ge1"], k["eq1"], k["gt1"]], N0, N1, ini),
             "o0": lambda: ts([k["sR0"]] + a_k, T.ot[:, 0:4 * NE:2], T.kq[:], r0, OP.is_equal),
             "o1": lambda: ts([k["s1"]], T.ot[:, 1:4 * NE:2], T.kq[:], r1, OP.is_equal),
             "a0": lambda: ts([k["sR0"]] + a_b, T.xf[:, 0:8], T.below[:], r0, OP.is_gt, r0, OP.mult),
             "a1": lambda: ts([k["s1"]], T.xf[:, 8:12], T.below[:, 4:8], r1, OP.is_gt, r1, OP.mult),
-            "b0": lambda: ts([k["sR0"], i_zx, a_hf] + a_b, T.stile[:, 4 * P + 2:4 * P + 32:4], T.above[:], r0, OP.is_le, hf, OP.mult),
-            "b1": lambda: ts([k["s1"], a_h1], T.stile[:, 4 * P + 34:4 * P + 48:4], T.above[:, 4:8], r1, OP.is_le, h1, OP.mult),
-            "hi": lambda: ts([k["a0"], k["a1"], i_zx], X[0], T.xf[:], big, OP.add, big, OP.subtract),
-            "lo": lambda: run("tt", [k["hi"]], X[1], T.xf[:], X[0], OP.subtract),
+            "b0": lambda: ts([k["sR0"], i_zx, a_hf] + a_b, T.xt[:, 2:32:4], T.above[:], r0, OP.is_le, hf, OP.mult),
+            "b1": lambda: ts([k["s1"], a_h1], T.xt[:, 34:48:4], T.above[:, 4:8], r1, OP.is_le, h1, OP.mult),
+            "hi": lambda: ts([k["a0"], k["a1"], i_zx], T.xt[:, 0:48:4], T.xf[:], big, OP.add, big, OP.subtract),
+            "lo": lambda: run("tt", [k["hi"]], T.xt[:, 1:48:4], T.xf[:], T.xt[:, 0:48:4], OP.subtract),
             "qo": onehots,
+            "qx": lists,
             "es": lambda: run("scan", [k["me"], k["mf"]], T.es[:], psZ[0][:, 0:NE], T.me[:], 0.0, OP.add, OP.mult),
-            "qs": lambda: quant(aS + [k["lo"], k["b0"], k["b1"]], S, T.stile[:]),
-            "eo": lambda: ts([k["es"]], eo[:, 0:3], T.es[:, 16:NE:17], 1 / up, OP.mult),
+            "qs": lambda: quant(aS, S, T.stile[:]),
+            "eo": lambda: ts([k["es"]], eo, T.es[:, 16:NE:17], 1 / up, OP.mult),
             "pick": chosen,
         }
         for s in RANKS.split() + LISTS.split():
             k[s] = calls[s]()
             if t == 0 and s == "gt0":
-                k["e3"] = ts([a_lf], T.eo[:, 3:4], T.lf[:], 11.0, OP.min, float(P), OP.add)
                 k["mf"] = run("tt", [a_1, a_r], T.me[:], T.m2[:], T.es[:], OP.add)
         vp, ap, ve = k["pick"], k["ap"], k["es"]
-        da, db = win("A", t, P, SND), win("B", t, P, SND)
-        send([vp], msg[0].bitcast(dt.uint8), da[0].bitcast(dt.uint8), db[0].bitcast(dt.uint8), t)
-        send([ap], msg[1], da[1], db[1], t)
+        send([vp, ap], H, "r", t, P, P + K)
         ach = [run("act", [ve], T.chs[0:1, K * t + 16 * m:K * t + 16 * m + 16], psZ[0][0:1, 17 * m + 1:17 * m + 17], AF.Copy)
                for m in range(3)]
         chtok.append(ach[-1])
@@ -302,17 +316,17 @@ def rank_program(g, core, T, topo):
             axo = run("act", [q1], T.xout[:], XS[R][:], AF.Copy)
             store("s", [axo], T.xe[:], T.xout[:])
 
-        def places(c, deps, bank):
-            m = mm(deps + [k_cs], bank[:, 0:128], CS, win(c, t, SND - 128, SND))
-            return lambda: ts([m], T["so%s%d" % (c, t)][:], bank[:, 116:128], T.lf[:], OP.add)
+        def places(c, deps, bank, tile):
+            m = mm(deps + [k_cs], bank[:, 0:128], CS, tile)
+            return lambda: ts([m], T["so%s%d" % (c, t)][:], bank[:, 0:12], T.lf[:], OP.add)
 
-        def pick(c, deps):
-            so, d, w = T["so%s%d" % (c, t)], win(c, t + 1, 0, P), cols("w%s%d" % (c, t), 0, SND)
-            return [run("copy", deps, d[0].bitcast(dt.uint32), w[0].bitcast(dt.uint32).indirect(so[:])),
-                    run("act", deps, d[1], w[1].indirect(so[:]), AF.Copy)]
+        def pick(c, deps, a=0, b=P):
+            so, d, w = T["so%s%d" % (c, t)][:, a // 16:b // 16], win(c, t + 1, a, b), win(c, t, 0, P + K)
+            return [run("copy", deps, d[0].bitcast(dt.uint32), w[0].bitcast(dt.uint32).indirect(so)),
+                    run("act", deps, d[1], w[1].indirect(so), AF.Copy)]
 
-        vsh = places("H", [vp, ap, ac0], psZ[1])()
-        sh["H"] = pick("H", [vsh])
+        vsh = places("H", [k["qx"], ac0], psZ[1], XQ)()
+        sh["H"] = pick("H", [vsh, vp, ap])
         for b, d in enumerate((ar1, ac1, aS[2], aS[3])):
             free["H", b] = [d]
         if not last:
@@ -320,16 +334,21 @@ def rank_program(g, core, T, topo):
         else:
             k_w = quant([lw], cols("wq", 0, 128), T.tw[:])
             store("s", sh["H"][:1], T.oc[:, 4 * P:8 * P], T.fin[:, P:2 * P].bitcast(dt.uint8))
-        ra, rb = ("rA%d" % t, got["A"]), ("rB%d" % t, got["B"])
-        la = places("A", [ra, aS[0]], psZ[2])
-        lb = places("B", [rb, aS[1]], psZ[3])
-        vsa = la()
-        vsb = lb()
-        sh["A"] = pick("A", [vsa, ra])
-        sh["B"] = pick("B", [vsb, rb])
-        for b, d in enumerate((ach + [ve], [vsh], [vsa], [vsb])):
+        la = places("A", [("pA%d" % t, got["A"]), aS[0]], psZ[2], win("A", t, -12, 116))
+        lb = places("B", [("pB%d" % t, got["B"]), aS[1]], psZ[3], win("B", t, -12, 116))
+        vs = {"A": [la(), ("rA%d" % t, got["A"])]}
+        vs["B"] = [lb(), ("rB%d" % t, got["B"])]
+        for b, d in enumerate((ach + [ve], [vsh], vs["A"][:1], vs["B"][:1])):
             free["Z", b] = d
-        if not last:
+        if last:
+            for c in "AB":
+                sh[c] = pick(c, vs[c])
+        else:
+            for part, a, b in (("L", 0, L), ("R", L, P)):
+                for c in "AB":
+                    sh[c + part] = pick(c, vs[c], a, b)
+            for c in "AB":
+                sh[c] = sh[c + "L"] + sh[c + "R"]
             decode(t + 1, LATER)
 
     my = mm(sh["A"] + free["Z", 0] + [k_w], psZ[0][:, 0:P], cols("wq", 0, 128), win("A", R, 0, P))

@@ -5,22 +5,23 @@ P, K, R = 192, 48, 3
 L = 128
 BF, F32, U16, FP8, U8 = "bfloat16", "float32", "uint16", "float8_e4m3fn_x4", "uint8"
 W0 = 32
-N0, N1 = L + P, L + P + P + P - L
+N0, N1 = L + P + 2, L + P + P + P - L + 4
 NE = 51
 DRIFT = ("x0L x0R x1L d0L x1R x2L d1L x3L d2L d3L x2R x3R qL d0R d1R d2R d3R qR",
          "x0L x1L x2L T0 T1 T2 d0L x3L d1L d2L d3L x0R x1R qL x3R x2R d0R d1R d3R d2R qR")
 RANKS = "eq0 gt0 sL0 ge1 gR0 eq1 gt1 sR0 s1"
-LISTS = "a0 o0 a1 o1 b0 hi qo lo b1 qx es qs eo pick"
+LISTS = "a0 h0 o0 o1 a1 h1 qo lo qx es qs eo own pick"
+PLAN = (("cA sA cB sB", "cA sA cB sB"), ("cA sA cB sB", "cA sA cB sB"))
 FIRST = "A0 A1 A2 A3 B0 B1 B2 B3 H0 H1 h0 H2 h1 H3 h2 h3"
 LATER = "A0L A1L A2L B0L H0L B1L H1L B2L H2L A3 B3 H3"
 
 SCRATCH = {}
 SCRATCH.update({n: ("sbuf", [128, w], BF) for n, w in dict(
     x0=768, x1=768, x2=768, x3=768, tl=768, tc=768, tr=768, tu=4, tw=512, ub=512, idx=128, stq=516, stm=516, st1=516,
-    cet=512, cst=512, i16=512, k51=NE, kq=2 * NE, dtile=1024, stile=4 * P, xt=512, cmp=N1, mul=N1, acc=N1, ot=512,
+    cet=512, cst=512, i16=128, d16=128, kq=4 * NE, dtile=1024, stile=4 * P, xt=512, cmp=N1, mul=N1, acc=N1, ot=512,
     ini=2, hf=2, h1=2).items()})
 SCRATCH.update({n: ("sbuf", [128, w], F32) for n, w in dict(
-    npc=1, c16=8, s16=8, junk=8, bm=8, hp=1, lf=1, nlf=1, th=2, below=8, above=8, sab=192, aj=2, xf=12,
+    npc=1, c16=8, s16=8, junk=8, bm=8, hp=1, lf=1, nlf=1, th=2, below=12, nj=2, sab=192, aj=2, xf=12,
     i17=NE, m1=NE, m2=NE, me=NE, es=NE, chs=R * K, xout=768, yout=192).items()})
 SCRATCH["eo"] = ("sbuf", [128, 4], U16)
 _Q = dict(uq=128, wq=128, e1=512, eq=512, em=512, ce=128, cs=128, dq=256, oq=128, fin=3 * P)
@@ -37,7 +38,7 @@ for _b in range(4):
     SCRATCH["psH%d" % _b] = ("psum", [128, 512], F32)
 
 SEMAPHORES = (["sv", "sa", "st", "sg", "left", "lc", "ll", "lr", "lx", "lu", "lw", "out"]
-              + [_s + str(_t) for _t in range(R) for _s in ("rA", "rB", "pA", "pB")])
+              + [_s + str(_t) for _t in range(R) for _s in ("rA", "rB", "pA", "pB", "sA", "sB")])
 
 
 def rank_program(g, core, T, topo):
@@ -111,6 +112,7 @@ def rank_program(g, core, T, topo):
     U, DQ, CE, CS, OQ = cols("uq", 0, 128), cols("dq", 0, P), cols("ce", 0, 128), cols("cs", 0, 128), cols("oq", 0, 128)
     E = {c: [cols(c, 128 * b, 128 * b + 128) for b in range(4)] for c in ("e1", "eq", "em")}
     up = 2.0 ** 40
+    big = 1.5 * 2.0 ** 27
 
     ll = load("s", "ll", T.tl[:], T.hl[:])
     lu = load("a", "lu", T.tu[:], T.u[:, 0:4])
@@ -122,15 +124,15 @@ def rank_program(g, core, T, topo):
     i_c = iota(T.c16[:], [[0, 8]], 16, 0)
     i_p = iota(T.npc[:], [[0, 1]], -16, -1)
     i_s = run("select", [i_c], T.s16[:], T.c16[:], [[-16, 8]], OP.is_ge, 0.0, 0, 1)
-    i_k = iota(T.k51[:], [[16, 3], [1, 17]], P - 1, 0)
+    i_j = iota(T.nj[:], [[-64, 2]], 0, -1)
     i_bm = run("select", [i_s], T.bm[:], T.s16[:], [[16, 8]], OP.is_ge, 0.0, 15, -1)
-    i_k = run("select", [i_k], T.k51[:], T.k51[:], [[0, 3], [1, 17]], OP.is_gt, -64.0, 0, 0)
+    i_16 = iota(T.i16[:], [[0, 8], [1, 16]], 0, 0)
     i_17 = iota(T.i17[:], [[0, 3], [1, 17]], -1, 0)
     i_zd = iota(T.dtile[:, 4 * P:], [[0, 1024 - 4 * P]], 0, 0)
     i_m = iota(T.mul[:], [[0, N1]], 1, 0)
-    i_16 = iota(T.i16[:], [[0, 8], [1, 16], [0, 4]], 0, 0)
     i_m = [run("select", [i_m], T.mul[:, 0:L], T.mul[:, 0:L], [[1, L]], OP.not_equal, up, 0, -1),
            run("select", [i_m], T.mul[:, N0:N0 + 64], T.mul[:, N0:N0 + 64], [[1, 64]], OP.not_equal, up, 64, -1)]
+    a_k = [iota(T.kq[:, 2 * NE * h:2 * NE * (h + 1)], [[16, 3], [1, 17], [0, 2]], P - 1 - 64 * h, -1) for h in range(2)]
 
     c_z = run("fill", [], T.stq[:], 0.0)
     i_zo = run("fill", [], T.ot[:, 4 * NE:], 0.0)
@@ -155,20 +157,23 @@ def rank_program(g, core, T, topo):
     a_hf = lin([a_hp], hf, T.hp[:], bias=-16.0)
     a_h1 = lin([a_hp], h1, T.hp[:], bias=48.0)
     a_lf = lin([a_n], T.lf[:], T.nlf[:], scale=-1.0)
-    a_th = [lin([a_n], T.th[:, 0:1], T.nlf[:], 1 / 16, (P + K) / 16), lin([a_n], T.th[:, 1:2], T.nlf[:], 1 / 16, (P + K - 1024) / 16)]
-    a_in = lin([a_n], T.ini[:, 0:1], T.nlf[:], 1 / up, P / up)
-    a_k = [lin([a_n, i_k], T.kq[:, h:2 * NE:2], T.k51[:], bias=T.nlf[:]) for h in range(2)]
-    a_b = [lin(a_th + [i_bm], T.below[:], T.bm[:], T.th[:, 0:1]), lin(a_th + [i_bm], T.above[:], T.bm[:], T.th[:, 1:2], 1024.0)]
+    a_th = lin([i_j], T.th[:], T.nj[:], 1 / 16, (P + K) / 16)
+    a_in = lin([i_j], T.ini[:], T.nj[:], 1 / up, P / up)
+    a_g = [lin([i_j], T.cmp[:, N0 - 2 + i:N1:N1 - N0], T.nj[:], 0.0, big * (1 - 2 * i)) for i in range(2)]
+    a_c = run("act", [i_16, a_n], T.d16[:], T.i16[:], AF.Abs, bias=T.nlf[:])
+    a_b = [lin([a_th, i_bm], T.below[:, 0:8], T.bm[:], T.th[:, 0:1]), lin([a_th, i_bm], T.below[:, 8:12], T.bm[:, 4:8], T.th[:, 1:2])]
     a_e = [lin([i_idx, a_hf], T.cet[:, 0:512:4], T.idx[:], 0.0, hf),
            lin([i_idx, a_lf], T.cet[:, 2:512:4], T.idx[:], 0.0, T.lf[:]),
            lin([i_idx, a_h1], T.cet[64:128, 1:512:4], T.idx[64:128, :], 0.0, T.h1[64:128, 0:1]),
            lin([i_idx, a_lf], T.cet[64:128, 3:512:4], T.idx[64:128, :], 0.0, T.lf[64:128, :]),
            lin([c_q], T.cet[0:64, 1:512:2], T.stq[0:64, 0:256], 0.0)]
     a_s = run("act", [i_17, a_n], T.m1[:], T.i17[:], AF.Sign, bias=T.nlf[:])
-    i_zx = lin([c_q], T.xt[:], T.stq[:, 0:512], 0.0)
+    a_c = [run("act", [a_c], T.cst[:, t:512:4], T.d16[:], AF.Relu, bias=1.0, scale=-1.0) for t in range(4)]
     a_1 = run("act", [a_s], T.m2[:], T.m1[:], AF.Abs)
     a_r = run("act", [a_s], T.es[:], T.m1[:], AF.Relu)
+    i_zx = lin([c_q], T.xt[:], T.stq[:, 0:512], 0.0)
     a_1 = lin([a_1], T.m2[:], T.m2[:], -up, up)
+    i_zx = run("iota", [i_zx], T.xt[:, 2:48:4], [[2, 12]], 0, 0, allow_small_or_imprecise_dtypes=True)
 
     free = {(k, b): [] for b in range(4) for k in "ZH"}
     tH, tZ, k = {}, {}, {}
@@ -192,26 +197,32 @@ def rank_program(g, core, T, topo):
 
     decode(0, FIRST)
 
-    def send(deps, src, what, t, a, b):
-        for kind in range(2):
-            wait("g", [deps[kind]])
-            tr = []
-            for who, c, side in ((right, "A", 0), (left, "B", 1)):
-                rid, pid, _ = topo.addr(who)
-                eng = topo.engines(core, who)[side::2]
-                s, d = src[kind], win(c, t, a, b)[kind]
-                if kind == 0:
-                    s, d = s.bitcast(dt.uint8), d.bitcast(dt.uint8)
-                tr.append(RemoteDMATransfer(dst_ids=[DstId(rid=rid, pnc=pid)], dma_engine_mask=sum(1 << e for e in eng),
-                                            remote_sem=T.sem[what + c + str(t)], src=s, dst=d))
-                total["left"] += len(eng)
-            g.remote_dma_fused(tr, local_sem=T.sem.left)
+    def share(src, dst, call):
+        eng = topo.engines(src, dst)
+        return {"": eng, "<": eng[:len(eng) // 2], ">": eng[len(eng) // 2:]}[call[2:]]
 
-    got = {"A": 2 * len(topo.engines(left, core)[0::2]), "B": 2 * len(topo.engines(right, core)[1::2])}
+    def send(plan, deps, src, sems, t, a, b):
+        for call in plan.split():
+            kind, c = "cs".index(call[0]), call[1]
+            who = right if c == "A" else left
+            rid, pid, _ = topo.addr(who)
+            eng = share(core, who, call)
+            s, d = src[kind], win(c, t, a, b)[kind]
+            if kind == 0:
+                s, d = s.bitcast(dt.uint8), d.bitcast(dt.uint8)
+            wait("g", [deps[kind]])
+            g.remote_dma_fused([RemoteDMATransfer(dst_ids=[DstId(rid=rid, pnc=pid)], dma_engine_mask=sum(1 << e for e in eng),
+                                                  remote_sem=T.sem[sems[kind] + c + str(t)], src=s, dst=d)], local_sem=T.sem.left)
+            total["left"] += len(eng)
+
+    def landed(plan, sem, c, t, kinds):
+        who = left if c == "A" else right
+        return (sem + c + str(t), sum(len(share(who, core, call)) for call in plan.split() if call[0] in kinds and call[1] == c))
+
     chtok = []
 
     for t in range(R):
-        last = t == R - 1
+        last, plan = t == R - 1, PLAN[min(t, 1)]
         for s in DRIFT[min(t, 1)].split():
             c, e = (0, L) if s[-1] == "L" else (L, P)
             if s[0] == "T":
@@ -219,8 +230,13 @@ def rank_program(g, core, T, topo):
             elif s[0] == "q":
                 if t == 0 and c:
                     k["ce"] = quant(a_e, CE, T.cet[:])
+                if last:
+                    axo = run("act", [k["x%d%s" % (b, s[-1])] for b in range(4)], T.xout[:, 4 * c:4 * e], XS[R][:, 4 * c:4 * e], AF.Copy)
+                    store("s", [axo], T.xe[:, 4 * c:4 * e], T.xout[:, 4 * c:4 * e])
                 k[s] = quant([k["d%d%s" % (b, s[-1])] for b in range(4)] + ([i_zd] if c else []), cols("dq", c, c + L),
                              T.dtile[:, 4 * c:4 * c + 4 * L])
+                if t == 0 and c:
+                    k["cs"] = quant(a_c, CS, T.cst[:])
             else:
                 b = int(s[1])
                 part = slice(4 * c + b, 4 * e, 4)
@@ -251,9 +267,9 @@ def rank_program(g, core, T, topo):
             lw = load("s", "lw", T.tw[:], T.w[:])
         a0, a1 = T.aj[:, 0:1], T.aj[:, 1:2]
         s0, s1 = T.sab[:, 0:L], T.sab[:, L:P]
-        ini = T.ini[:, 0:1]
-        r0, r1 = T.acc[:, N0 - 1:N0], T.acc[:, N1 - 1:N1]
-        big = 1.5 * 2.0 ** 27
+        ini = T.ini[:, 0:1], T.ini[:, 1:2]
+        r0, r1 = T.acc[:, N0 - 3:N0 - 2], T.acc[:, N1 - 3:N1 - 2]
+        g0, g1 = T.acc[:, N0 - 1:N0], T.acc[:, N1 - 1:N1]
         S, XQ, eo, H = cols("sq%d" % t, 0, P), cols("xq%d" % t, 0, 128), T.eo[:, 0:3], win("H", t, P, P + K)
 
         def scan(deps, a, b, first):
@@ -264,9 +280,14 @@ def rank_program(g, core, T, topo):
             k["me"] = mm([q, k["ce"], ar0], psZ[0][:, 0:128], CE, OQ)
             return q
 
+        def places(c, deps, bank, tile):
+            m = mm(deps + [k["cs"]], bank[:, 0:128], CS, tile)
+            return lambda: ts([m, a_lf], T["so%s%d" % (c, t)][:], bank[:, 0:12], T.lf[:], OP.add)
+
         def lists():
-            q = quant([k["lo"], k["b0"], k["b1"]], XQ, T.xt[:])
-            send([q, q], cols("xq%d" % t, 0, 12), "p", t, -12, 0)
+            q = quant([k["lo"]], XQ, T.xt[:])
+            send(plan[0], [q, q], cols("xq%d" % t, 0, 12), "pp", t, -12, 0)
+            calls["own"] = places("H", [q, ac0], psZ[1], XQ)
             return q
 
         def chosen():
@@ -277,21 +298,20 @@ def rank_program(g, core, T, topo):
         calls = {
             "eq0": lambda: ts([ar0, ac0], T.cmp[:, 0:L], s0, a0, OP.is_equal, 1 / up, OP.mult),
             "gt0": lambda: ts([ar0, ac0], T.cmp[:, L:2 * L], s0, a0, OP.is_gt),
-            "gR0": lambda: ts([ar1, ac0], T.cmp[:, 2 * L:N0], s1, a0, OP.is_gt),
+            "gR0": lambda: ts([ar1, ac0], T.cmp[:, 2 * L:N0 - 2], s1, a0, OP.is_gt),
             "ge1": lambda: ts([ar0, ac1], T.cmp[:, N0 + 64:N0 + 64 + L], s0, a1, OP.is_ge),
             "eq1": lambda: ts([ar1, ac1], T.cmp[:, N0:N0 + 64], s1, a1, OP.is_equal, 1 / up, OP.mult),
-            "gt1": lambda: ts([ar1, ac1], T.cmp[:, N0 + 64 + L:N1], s1, a1, OP.is_gt),
-            "sL0": lambda: scan([k["eq0"], a_in] + i_m, 0, L, ini),
-            "sR0": lambda: scan([k["sL0"], k["gt0"], k["gR0"]], L, N0, T.acc[:, L - 1:L]),
-            "s1": lambda: scan([k["ge1"], k["eq1"], k["gt1"]], N0, N1, ini),
-            "o0": lambda: ts([k["sR0"]] + a_k, T.ot[:, 0:4 * NE:2], T.kq[:], r0, OP.is_equal),
-            "o1": lambda: ts([k["s1"]], T.ot[:, 1:4 * NE:2], T.kq[:], r1, OP.is_equal),
-            "a0": lambda: ts([k["sR0"]] + a_b, T.xf[:, 0:8], T.below[:], r0, OP.is_gt, r0, OP.mult),
-            "a1": lambda: ts([k["s1"]], T.xf[:, 8:12], T.below[:, 4:8], r1, OP.is_gt, r1, OP.mult),
-            "b0": lambda: ts([k["sR0"], i_zx, a_hf] + a_b, T.xt[:, 2:32:4], T.above[:], r0, OP.is_le, hf, OP.mult),
-            "b1": lambda: ts([k["s1"], a_h1], T.xt[:, 34:48:4], T.above[:, 4:8], r1, OP.is_le, h1, OP.mult),
-            "hi": lambda: ts([k["a0"], k["a1"], i_zx], T.xt[:, 0:48:4], T.xf[:], big, OP.add, big, OP.subtract),
-            "lo": lambda: run("tt", [k["hi"]], T.xt[:, 1:48:4], T.xf[:], T.xt[:, 0:48:4], OP.subtract),
+            "gt1": lambda: ts([ar1, ac1], T.cmp[:, N0 + 64 + L:N1 - 2], s1, a1, OP.is_gt),
+            "sL0": lambda: scan([k["eq0"], k["gt0"], a_in] + i_m, 0, 2 * L, ini[0]),
+            "sR0": lambda: scan([k["sL0"], k["gR0"]] + a_g, 2 * L, N0, T.acc[:, 2 * L - 1:2 * L]),
+            "s1": lambda: scan([k["ge1"], k["eq1"], k["gt1"], a_in] + i_m + a_g, N0, N1, ini[1]),
+            "o0": lambda: ts([k["sR0"]] + a_k, T.ot[:, 0:4 * NE:2], T.kq[:, 0:2 * NE], r0, OP.is_equal),
+            "o1": lambda: ts([k["s1"]] + a_k, T.ot[:, 1:4 * NE:2], T.kq[:, 2 * NE:], r1, OP.is_equal),
+            "a0": lambda: ts([k["sR0"]] + a_b, T.xf[:, 0:8], T.below[:, 0:8], r0, OP.is_gt, r0, OP.mult),
+            "a1": lambda: ts([k["s1"]] + a_b, T.xf[:, 8:12], T.below[:, 8:12], r1, OP.is_gt, r1, OP.mult),
+            "h0": lambda: ts([k["sR0"], i_zx] + a_b, T.xt[:, 0:32:4], T.below[:, 0:8], r0, OP.is_gt, g0, OP.mult),
+            "h1": lambda: ts([k["s1"], i_zx] + a_b, T.xt[:, 32:48:4], T.below[:, 8:12], r1, OP.is_gt, g1, OP.mult),
+            "lo": lambda: run("tt", [k["a0"], k["a1"], k["h0"], k["h1"]], T.xt[:, 1:48:4], T.xf[:], T.xt[:, 0:48:4], OP.subtract),
             "qo": onehots,
             "qx": lists,
             "es": lambda: run("scan", [k["me"], k["mf"]], T.es[:], psZ[0][:, 0:NE], T.me[:], 0.0, OP.add, OP.mult),
@@ -304,49 +324,40 @@ def rank_program(g, core, T, topo):
             if t == 0 and s == "gt0":
                 k["mf"] = run("tt", [a_1, a_r], T.me[:], T.m2[:], T.es[:], OP.add)
         vp, ap, ve = k["pick"], k["ap"], k["es"]
-        send([vp, ap], H, "r", t, P, P + K)
+        send(plan[1], [vp, ap], H, "rs", t, P, P + K)
+
+        def pick(c, deps, a=0, b=P, codes=(), scales=()):
+            so, d, w = T["so%s%d" % (c, t)][:, a // 16:b // 16], win(c, t + 1, a, b), win(c, t, 0, P + K)
+            return [run("copy", deps + list(codes), d[0].bitcast(dt.uint32), w[0].bitcast(dt.uint32).indirect(so)),
+                    run("act", deps + list(scales), d[1], w[1].indirect(so), AF.Copy)]
+
+        vsh = k["own"]
+        sh["H"] = pick("H", [vsh], codes=[vp], scales=[ap])
+        for b, d in enumerate((ar1, ac1, aS[2], aS[3])):
+            free["H", b] = [d]
+        la = places("A", [landed(plan[0], "p", "A", t, "cs"), aS[0]], psZ[2], win("A", t, -12, 116))
+        lb = places("B", [landed(plan[0], "p", "B", t, "cs"), aS[1]], psZ[3], win("B", t, -12, 116))
         ach = [run("act", [ve], T.chs[0:1, K * t + 16 * m:K * t + 16 * m + 16], psZ[0][0:1, 17 * m + 1:17 * m + 17], AF.Copy)
                for m in range(3)]
         chtok.append(ach[-1])
-        if t == 0:
-            v_c = ts([i_16, a_lf], T.cst[:], T.i16[:], T.lf[:], OP.is_equal)
-            k_cs = quant([v_c], CS, T.cst[:])
-        if last:
-            store("s", chtok, T.ch[:], T.chs[0:1, :])
-            axo = run("act", [q1], T.xout[:], XS[R][:], AF.Copy)
-            store("s", [axo], T.xe[:], T.xout[:])
-
-        def places(c, deps, bank, tile):
-            m = mm(deps + [k_cs], bank[:, 0:128], CS, tile)
-            return lambda: ts([m], T["so%s%d" % (c, t)][:], bank[:, 0:12], T.lf[:], OP.add)
-
-        def pick(c, deps, a=0, b=P):
-            so, d, w = T["so%s%d" % (c, t)][:, a // 16:b // 16], win(c, t + 1, a, b), win(c, t, 0, P + K)
-            return [run("copy", deps, d[0].bitcast(dt.uint32), w[0].bitcast(dt.uint32).indirect(so)),
-                    run("act", deps, d[1], w[1].indirect(so), AF.Copy)]
-
-        vsh = places("H", [k["qx"], ac0], psZ[1], XQ)()
-        sh["H"] = pick("H", [vsh, vp, ap])
-        for b, d in enumerate((ar1, ac1, aS[2], aS[3])):
-            free["H", b] = [d]
         if not last:
             decode(t + 1, "h0 h1 h2 h3")
         else:
-            k_w = quant([lw], cols("wq", 0, 128), T.tw[:])
+            store("s", chtok, T.ch[:], T.chs[0:1, :])
             store("s", sh["H"][:1], T.oc[:, 4 * P:8 * P], T.fin[:, P:2 * P].bitcast(dt.uint8))
-        la = places("A", [("pA%d" % t, got["A"]), aS[0]], psZ[2], win("A", t, -12, 116))
-        lb = places("B", [("pB%d" % t, got["B"]), aS[1]], psZ[3], win("B", t, -12, 116))
-        vs = {"A": [la(), ("rA%d" % t, got["A"])]}
-        vs["B"] = [lb(), ("rB%d" % t, got["B"])]
+        if t == 0:
+            k_w = quant([lw], cols("wq", 0, 128), T.tw[:])
+        vs = {"A": [la()], "B": [lb()]}
+        arr = {c: [[landed(plan[1], "r", c, t, "c")], [landed(plan[1], "s", c, t, "s")]] for c in "AB"}
         for b, d in enumerate((ach + [ve], [vsh], vs["A"][:1], vs["B"][:1])):
             free["Z", b] = d
         if last:
             for c in "AB":
-                sh[c] = pick(c, vs[c])
+                sh[c] = pick(c, vs[c], 0, P, *arr[c])
         else:
             for part, a, b in (("L", 0, L), ("R", L, P)):
                 for c in "AB":
-                    sh[c + part] = pick(c, vs[c], a, b)
+                    sh[c + part] = pick(c, vs[c], a, b, *arr[c])
             for c in "AB":
                 sh[c] = sh[c + "L"] + sh[c + "R"]
             decode(t + 1, LATER)

from concourse.bass import DstId, RemoteDMATransfer
from concourse.mybir import dt, AluOpType as OP, ActivationFunctionType as AF

P, K, R = 192, 48, 3
L = 128
BF, F32, U16, FP8, U8 = "bfloat16", "float32", "uint16", "float8_e4m3fn_x4", "uint8"
W0 = 32
N0, N1 = L + P + 2, L + P + P + P - L + 4
NE = 51
DRIFT = ("x0L x0R x1L d0L x1R x2L d1L x3L d2L d3L x2R x3R qL d0R d1R d2R d3R qR",
         "x0L x1L x2L T0 T1 T2 d0L x3L d1L d2L d3L x0R x1R qL x3R x2R d0R d1R d3R d2R qR")
RANKS = "eq0 gt0 sL0 ge1 gR0 eq1 gt1 sR0 s1"
LISTS = "a0 h0 o0 o1 a1 h1 qo lo qx es qs eo own pick"
PLAN = (("cA sA cB sB", "cA sA cB sB"), ("cA sA cB sB", "cA sA cB sB"))
FIRST = "A0 A1 A2 A3 B0 B1 B2 B3 H0 H1 h0 H2 h1 H3 h2 h3"
LATER = "A0L A1L A2L B0L H0L B1L H1L B2L H2L A3 B3 H3"

SCRATCH = {}
SCRATCH.update({n: ("sbuf", [128, w], BF) for n, w in dict(
    x0=768, x1=768, x2=768, x3=768, tl=768, tc=768, tr=768, tu=4, tw=512, ub=512, idx=128, stq=516, stm=516, st1=516,
    cet=512, cst=512, i16=128, d16=128, kq=4 * NE, dtile=1024, stile=4 * P, xt=512, cmp=N1, mul=N1, acc=N1, ot=512,
    ini=2, hf=2, h1=2).items()})
SCRATCH.update({n: ("sbuf", [128, w], F32) for n, w in dict(
    npc=1, c16=8, s16=8, junk=8, bm=8, hp=1, lf=1, nlf=1, th=2, below=12, nj=2, sab=192, aj=2, xf=12,
    i17=NE, m1=NE, m2=NE, me=NE, es=NE, chs=R * K, xout=768, yout=192).items()})
SCRATCH["eo"] = ("sbuf", [128, 4], U16)
_Q = dict(uq=128, wq=128, e1=512, eq=512, em=512, ce=128, cs=128, dq=256, oq=128, fin=3 * P)
for _t in range(R):
    _Q.update({"sq%d" % _t: P, "xq%d" % _t: 128})
    for _n in "AHB":
        _Q["w%s%d" % (_n, _t)] = W0 + P + K
        SCRATCH["so%s%d" % (_n, _t)] = ("sbuf", [128, 12], U16)
for _n, _w in _Q.items():
    SCRATCH[_n] = ("sbuf", [128, _w], FP8)
    SCRATCH[_n + "_s"] = ("sbuf", [128, _w], U8)
for _b in range(4):
    SCRATCH["psZ%d" % _b] = ("psum", [128, 512], F32)
    SCRATCH["psH%d" % _b] = ("psum", [128, 512], F32)

SEMAPHORES = (["sv", "sa", "st", "sg", "left", "lc", "ll", "lr", "lx", "lu", "lw", "out"]
              + [_s + str(_t) for _t in range(R) for _s in ("rA", "rB", "pA", "pB", "sA", "sB")])


def rank_program(g, core, T, topo):
    rank = T.rank_of(core)
    if rank is None:
        return
    n = len(T.cores)
    right, left = T.cores[(rank + 1) % n], T.cores[(rank - 1) % n]
    Q = {"v": g.vector, "a": g.scalar, "t": g.tensor, "g": g, "s": g.sync}
    cnt = {"v": 0, "a": 0, "t": 0, "g": 0}
    seen = {q: {} for q in Q}
    total = {"out": 0, "left": 0}

    def wait(q, deps):
        need = {}
        for s, v in deps:
            need[s] = max(v, need.get(s, 0))
        for s, v in need.items():
            if seen[q].get(s, 0) < v:
                Q[q].wait_ge(T.sem[s], v)
                seen[q][s] = v

    CALLS = {"act": g.scalar.activation, "mm": g.tensor.matmul_mx, "quant": g.vector.quantize_mx, "copy": g.vector.tensor_copy,
             "tt": g.vector.tensor_tensor, "ts": g.vector.tensor_scalar, "scan": g.vector.tensor_tensor_scan,
             "fill": g.vector.memset, "iota": g.iota, "select": g.affine_select}
    QUEUE = {"act": "a", "mm": "t", "iota": "g", "select": "g"}

    def run(name, deps, *args, **kw):
        q = QUEUE.get(name, "v")
        wait(q, deps)
        CALLS[name](*args, **kw).then_inc(T.sem["s" + q], 1)
        cnt[q] += 1
        return ("s" + q, cnt[q])

    def load(q, sem, out, in_):
        Q[q].dma_start(out, in_).then_inc(T.sem[sem], 16)
        return (sem, 16)

    def store(q, deps, out, in_):
        wait(q, deps)
        Q[q].dma_start(out, in_).then_inc(T.sem.out, 16)
        total["out"] += 16

    def ts(deps, out, in0, s1, op0, s2=None, op1=None):
        kw = {} if op1 is None else {"op1": op1}
        return run("ts", deps, out=out, in0=in0, scalar1=s1, scalar2=s2, op0=op0, **kw)

    def lin(deps, out, in_, scale=1.0, bias=0.0):
        return run("act", deps, out, in_, AF.Identity, bias=bias, scale=scale)

    def iota(out, pattern, base, step):
        return run("iota", [], out, pattern, base, step, allow_small_or_imprecise_dtypes=True)

    def cols(name, a, b):
        return T[name][:, a:b], T[name + "_s"][:, a:b]

    def win(k, t, a, b):
        o = P * "AHB".index(k)
        return cols("fin", o + a, o + b) if t == R else cols("w%s%d" % (k, t), W0 + a, W0 + b)

    def mm(deps, out, l, r, start=True, stop=True):
        return run("mm", deps, out, l[0], l[1], r[0], r[1], start, stop)

    def quant(deps, q, tile):
        return run("quant", deps, q[0], q[1], tile)

    psZ = [T["psZ%d" % b] for b in range(4)]
    psH = [T["psH%d" % b] for b in range(4)]
    psS = [psZ[2], psZ[3], psH[2], psH[3]]
    XS = [T.x0, T.x1, T.x2, T.x3]
    U, DQ, CE, CS, OQ = cols("uq", 0, 128), cols("dq", 0, P), cols("ce", 0, 128), cols("cs", 0, 128), cols("oq", 0, 128)
    E = {c: [cols(c, 128 * b, 128 * b + 128) for b in range(4)] for c in ("e1", "eq", "em")}
    up = 2.0 ** 40
    big = 1.5 * 2.0 ** 27

    ll = load("s", "ll", T.tl[:], T.hl[:])
    lu = load("a", "lu", T.tu[:], T.u[:, 0:4])
    lr = load("a", "lr", T.tr[:], T.hr[:])
    lc = load("s", "lc", T.tc[:], T.hc[:])
    lx = load("s", "lx", T.x0[:], T.x[:])

    i_idx = iota(T.idx[:], [[1, 128]], 0, -1)
    i_c = iota(T.c16[:], [[0, 8]], 16, 0)
    i_p = iota(T.npc[:], [[0, 1]], -16, -1)
    i_s = run("select", [i_c], T.s16[:], T.c16[:], [[-16, 8]], OP.is_ge, 0.0, 0, 1)
    i_j = iota(T.nj[:], [[-64, 2]], 0, -1)
    i_bm = run("select", [i_s], T.bm[:], T.s16[:], [[16, 8]], OP.is_ge, 0.0, 15, -1)
    i_16 = iota(T.i16[:], [[0, 8], [1, 16]], 0, 0)
    i_17 = iota(T.i17[:], [[0, 3], [1, 17]], -1, 0)
    i_zd = iota(T.dtile[:, 4 * P:], [[0, 1024 - 4 * P]], 0, 0)
    i_m = iota(T.mul[:], [[0, N1]], 1, 0)
    i_m = [run("select", [i_m], T.mul[:, 0:L], T.mul[:, 0:L], [[1, L]], OP.not_equal, up, 0, -1),
           run("select", [i_m], T.mul[:, N0:N0 + 64], T.mul[:, N0:N0 + 64], [[1, 64]], OP.not_equal, up, 64, -1)]
    a_k = [iota(T.kq[:, 2 * NE * h:2 * NE * (h + 1)], [[16, 3], [1, 17], [0, 2]], P - 1 - 64 * h, -1) for h in range(2)]

    c_z = run("fill", [], T.stq[:], 0.0)
    i_zo = run("fill", [], T.ot[:, 4 * NE:], 0.0)
    c_q = ts([c_z, i_idx], T.stq[:, 3:515:4], T.idx[:], 0.0, OP.is_equal, 0.25, OP.mult)
    c_m = run("act", [c_q], T.stm[:], T.stq[:], AF.Copy, scale=-2.0)
    c_1 = run("act", [c_q], T.st1[:], T.stq[:], AF.Copy, scale=4.0)
    u4 = [lin([lu], T.ub[:, t:512:4], T.idx[:], 0.0, T.tu[:, t:t + 1]) for t in range(4)]

    def strips(c, d, strip):
        return [quant([d], E[c][b], strip[:, 3 - b:515 - b]) for b in range(4)]

    kE = {"eq": strips("eq", c_q, T.stq), "em": strips("em", c_m, T.stm)}
    sh = {"A": [quant([ll], win("A", 0, 0, P), T.tl[:])]}
    k_u = quant(u4, U, T.ub[:])
    sh["B"] = [quant([lr], win("B", 0, 0, P), T.tr[:])]
    sh["H"] = [quant([lc], win("H", 0, 0, P), T.tc[:])]
    kE["e1"] = strips("e1", c_1, T.st1)

    hf, h1 = T.hf[:, 0:1], T.h1[:, 0:1]
    a_hp = run("act", [i_s], T.junk[:], T.s16[:], AF.Identity, accum_out=T.hp[:])
    a_n = lin([a_hp, i_p], T.nlf[:], T.hp[:], bias=T.npc[:])
    a_hf = lin([a_hp], hf, T.hp[:], bias=-16.0)
    a_h1 = lin([a_hp], h1, T.hp[:], bias=48.0)
    a_lf = lin([a_n], T.lf[:], T.nlf[:], scale=-1.0)
    a_th = lin([i_j], T.th[:], T.nj[:], 1 / 16, (P + K) / 16)
    a_in = lin([i_j], T.ini[:], T.nj[:], 1 / up, P / up)
    a_g = [lin([i_j], T.cmp[:, N0 - 2 + i:N1:N1 - N0], T.nj[:], 0.0, big * (1 - 2 * i)) for i in range(2)]
    a_c = run("act", [i_16, a_n], T.d16[:], T.i16[:], AF.Abs, bias=T.nlf[:])
    a_b = [lin([a_th, i_bm], T.below[:, 0:8], T.bm[:], T.th[:, 0:1]), lin([a_th, i_bm], T.below[:, 8:12], T.bm[:, 4:8], T.th[:, 1:2])]
    a_e = [lin([i_idx, a_hf], T.cet[:, 0:512:4], T.idx[:], 0.0, hf),
           lin([i_idx, a_lf], T.cet[:, 2:512:4], T.idx[:], 0.0, T.lf[:]),
           lin([i_idx, a_h1], T.cet[64:128, 1:512:4], T.idx[64:128, :], 0.0, T.h1[64:128, 0:1]),
           lin([i_idx, a_lf], T.cet[64:128, 3:512:4], T.idx[64:128, :], 0.0, T.lf[64:128, :]),
           lin([c_q], T.cet[0:64, 1:512:2], T.stq[0:64, 0:256], 0.0)]
    a_s = run("act", [i_17, a_n], T.m1[:], T.i17[:], AF.Sign, bias=T.nlf[:])
    a_c = [run("act", [a_c], T.cst[:, t:512:4], T.d16[:], AF.Relu, bias=1.0, scale=-1.0) for t in range(4)]
    a_1 = run("act", [a_s], T.m2[:], T.m1[:], AF.Abs)
    a_r = run("act", [a_s], T.es[:], T.m1[:], AF.Relu)
    i_zx = lin([c_q], T.xt[:], T.stq[:, 0:512], 0.0)
    a_1 = lin([a_1], T.m2[:], T.m2[:], -up, up)
    i_zx = run("iota", [i_zx], T.xt[:, 2:48:4], [[2, 12]], 0, 0, allow_small_or_imprecise_dtypes=True)

    free = {(k, b): [] for b in range(4) for k in "ZH"}
    tH, tZ, k = {}, {}, {}

    def decode(t, steps):
        for w in steps.split():
            c, b, part = w[0], int(w[1]), w[2:]
            a, e = {"": (0, P), "L": (0, L), "R": (P - L, P)}[part]
            if c == "h":
                tH[b] = mm(sh["H"] + free["H", b] + [kE["e1"][b]], psH[b][:, 0:P], E["e1"][b], win("H", t, 0, P))
                continue
            tile = "em" if c == "H" else "eq"
            deps = [kE[tile][b]] + sh[c if c == "H" else c + part]
            if c == "A":
                deps = deps + ([k["x%dL" % b]] if part == "R" else free["Z", b])
            m = mm(deps, psZ[b][:, 0:e - a], E[tile][b], win(c, t, a, e), c == "A", c == "H")
            if c == "H":
                for p, c0, c1 in (("L", 0, L), ("R", L, P)):
                    if part in ("", p):
                        tZ[b, p] = (m, psZ[b][:, c0 - a:c1 - a])

    decode(0, FIRST)

    def share(src, dst, call):
        eng = topo.engines(src, dst)
        return {"": eng, "<": eng[:len(eng) // 2], ">": eng[len(eng) // 2:]}[call[2:]]

    def send(plan, deps, src, sems, t, a, b):
        for call in plan.split():
            kind, c = "cs".index(call[0]), call[1]
            who = right if c == "A" else left
            rid, pid, _ = topo.addr(who)
            eng = share(core, who, call)
            s, d = src[kind], win(c, t, a, b)[kind]
            if kind == 0:
                s, d = s.bitcast(dt.uint8), d.bitcast(dt.uint8)
            wait("g", [deps[kind]])
            g.remote_dma_fused([RemoteDMATransfer(dst_ids=[DstId(rid=rid, pnc=pid)], dma_engine_mask=sum(1 << e for e in eng),
                                                  remote_sem=T.sem[sems[kind] + c + str(t)], src=s, dst=d)], local_sem=T.sem.left)
            total["left"] += len(eng)

    def landed(plan, sem, c, t, kinds):
        who = left if c == "A" else right
        return (sem + c + str(t), sum(len(share(who, core, call)) for call in plan.split() if call[0] in kinds and call[1] == c))

    chtok = []

    for t in range(R):
        last, plan = t == R - 1, PLAN[min(t, 1)]
        for s in DRIFT[min(t, 1)].split():
            c, e = (0, L) if s[-1] == "L" else (L, P)
            if s[0] == "T":
                decode(t, "A%sR B%sR H%sR" % (s[1], s[1], s[1]))
            elif s[0] == "q":
                if t == 0 and c:
                    k["ce"] = quant(a_e, CE, T.cet[:])
                if last:
                    axo = run("act", [k["x%d%s" % (b, s[-1])] for b in range(4)], T.xout[:, 4 * c:4 * e], XS[R][:, 4 * c:4 * e], AF.Copy)
                    store("s", [axo], T.xe[:, 4 * c:4 * e], T.xout[:, 4 * c:4 * e])
                k[s] = quant([k["d%d%s" % (b, s[-1])] for b in range(4)] + ([i_zd] if c else []), cols("dq", c, c + L),
                             T.dtile[:, 4 * c:4 * c + 4 * L])
                if t == 0 and c:
                    k["cs"] = quant(a_c, CS, T.cst[:])
            else:
                b = int(s[1])
                part = slice(4 * c + b, 4 * e, 4)
                if s[0] == "x":
                    m, z = tZ[b, s[-1]]
                    k[s] = run("tt", [m, lx], XS[t + 1][:, part], z, XS[t][:, part], OP.add)
                else:
                    k[s] = run("tt", [k["x" + s[1:]], tH[b]], T.dtile[:, part], XS[t + 1][:, part], psH[b][:, c:e], OP.subtract)
        q0, q1 = k["qL"], k["qR"]
        mr0 = mm([q0, k_u, k["x0R"]], psZ[0][:, 0:L], U, cols("dq", 0, L))
        mc0 = mm([q0, k["x1R"]], psZ[1][:, 0:128], cols("dq", 0, L), U)
        for b in range(2):
            mm([k["x%dR" % (2 + b)]], psS[b][:, 0:P], E["e1"][b], win("H", t, 0, P), True, False)
        mc1 = mm([q1], psH[1][:, 0:128], cols("dq", 64, P), U)
        mr1 = mm([q1], psH[0][:, 0:L], U, cols("dq", L, 2 * L))
        mS = []
        for b in range(4):
            if b >= 2:
                mm([q1], psS[b][:, 0:P], E["e1"][b], win("H", t, 0, P), True, False)
            mS.append(mm([q1], psS[b][:, 0:P], E["e1"][b], DQ, False, True))
        ar0 = run("act", [mr0], T.sab[:, 0:L], psZ[0][:, 0:L], AF.Abs)
        ac0 = run("act", [mc0], T.aj[:, 0:1], psZ[1][:, 0:1], AF.Abs)
        ac1 = run("act", [mc1], T.aj[:, 1:2], psH[1][:, 0:1], AF.Abs)
        ar1 = run("act", [mr1], T.sab[:, L:P], psH[0][:, 0:P - L], AF.Abs)
        aS = [run("act", [mS[b]], T.stile[:, b:4 * P:4], psS[b][:, 0:P], AF.Copy) for b in range(4)]
        if t == 0:
            wait("s", [q0])
            lw = load("s", "lw", T.tw[:], T.w[:])
        a0, a1 = T.aj[:, 0:1], T.aj[:, 1:2]
        s0, s1 = T.sab[:, 0:L], T.sab[:, L:P]
        ini = T.ini[:, 0:1], T.ini[:, 1:2]
        r0, r1 = T.acc[:, N0 - 3:N0 - 2], T.acc[:, N1 - 3:N1 - 2]
        g0, g1 = T.acc[:, N0 - 1:N0], T.acc[:, N1 - 1:N1]
        S, XQ, eo, H = cols("sq%d" % t, 0, P), cols("xq%d" % t, 0, 128), T.eo[:, 0:3], win("H", t, P, P + K)

        def scan(deps, a, b, first):
            return run("scan", deps, T.acc[:, a:b], T.mul[:, a:b], T.cmp[:, a:b], first, OP.mult, OP.add)

        def onehots():
            q = quant([k["o0"], k["o1"], i_zo], OQ, T.ot[:])
            k["me"] = mm([q, k["ce"], ar0], psZ[0][:, 0:128], CE, OQ)
            return q

        def places(c, deps, bank, tile):
            m = mm(deps + [k["cs"]], bank[:, 0:128], CS, tile)
            return lambda: ts([m, a_lf], T["so%s%d" % (c, t)][:], bank[:, 0:12], T.lf[:], OP.add)

        def lists():
            q = quant([k["lo"]], XQ, T.xt[:])
            send(plan[0], [q, q], cols("xq%d" % t, 0, 12), "pp", t, -12, 0)
            calls["own"] = places("H", [q, ac0], psZ[1], XQ)
            return q

        def chosen():
            deps = [k["eo"], k["qs"]]
            k["ap"] = run("act", deps, H[1], S[1].indirect(eo), AF.Copy)
            return run("copy", deps, H[0].bitcast(dt.uint32), S[0].bitcast(dt.uint32).indirect(eo))

        calls = {
            "eq0": lambda: ts([ar0, ac0], T.cmp[:, 0:L], s0, a0, OP.is_equal, 1 / up, OP.mult),
            "gt0": lambda: ts([ar0, ac0], T.cmp[:, L:2 * L], s0, a0, OP.is_gt),
            "gR0": lambda: ts([ar1, ac0], T.cmp[:, 2 * L:N0 - 2], s1, a0, OP.is_gt),
            "ge1": lambda: ts([ar0, ac1], T.cmp[:, N0 + 64:N0 + 64 + L], s0, a1, OP.is_ge),
            "eq1": lambda: ts([ar1, ac1], T.cmp[:, N0:N0 + 64], s1, a1, OP.is_equal, 1 / up, OP.mult),
            "gt1": lambda: ts([ar1, ac1], T.cmp[:, N0 + 64 + L:N1 - 2], s1, a1, OP.is_gt),
            "sL0": lambda: scan([k["eq0"], k["gt0"], a_in] + i_m, 0, 2 * L, ini[0]),
            "sR0": lambda: scan([k["sL0"], k["gR0"]] + a_g, 2 * L, N0, T.acc[:, 2 * L - 1:2 * L]),
            "s1": lambda: scan([k["ge1"], k["eq1"], k["gt1"], a_in] + i_m + a_g, N0, N1, ini[1]),
            "o0": lambda: ts([k["sR0"]] + a_k, T.ot[:, 0:4 * NE:2], T.kq[:, 0:2 * NE], r0, OP.is_equal),
            "o1": lambda: ts([k["s1"]] + a_k, T.ot[:, 1:4 * NE:2], T.kq[:, 2 * NE:], r1, OP.is_equal),
            "a0": lambda: ts([k["sR0"]] + a_b, T.xf[:, 0:8], T.below[:, 0:8], r0, OP.is_gt, r0, OP.mult),
            "a1": lambda: ts([k["s1"]] + a_b, T.xf[:, 8:12], T.below[:, 8:12], r1, OP.is_gt, r1, OP.mult),
            "h0": lambda: ts([k["sR0"], i_zx] + a_b, T.xt[:, 0:32:4], T.below[:, 0:8], r0, OP.is_gt, g0, OP.mult),
            "h1": lambda: ts([k["s1"], i_zx] + a_b, T.xt[:, 32:48:4], T.below[:, 8:12], r1, OP.is_gt, g1, OP.mult),
            "lo": lambda: run("tt", [k["a0"], k["a1"], k["h0"], k["h1"]], T.xt[:, 1:48:4], T.xf[:], T.xt[:, 0:48:4], OP.subtract),
            "qo": onehots,
            "qx": lists,
            "es": lambda: run("scan", [k["me"], k["mf"]], T.es[:], psZ[0][:, 0:NE], T.me[:], 0.0, OP.add, OP.mult),
            "qs": lambda: quant(aS, S, T.stile[:]),
            "eo": lambda: ts([k["es"]], eo, T.es[:, 16:NE:17], 1 / up, OP.mult),
            "pick": chosen,
        }
        for s in RANKS.split() + LISTS.split():
            k[s] = calls[s]()
            if t == 0 and s == "gt0":
                k["mf"] = run("tt", [a_1, a_r], T.me[:], T.m2[:], T.es[:], OP.add)
        vp, ap, ve = k["pick"], k["ap"], k["es"]
        send(plan[1], [vp, ap], H, "rs", t, P, P + K)

        def pick(c, deps, a=0, b=P, codes=(), scales=()):
            so, d, w = T["so%s%d" % (c, t)][:, a // 16:b // 16], win(c, t + 1, a, b), win(c, t, 0, P + K)
            return [run("copy", deps + list(codes), d[0].bitcast(dt.uint32), w[0].bitcast(dt.uint32).indirect(so)),
                    run("act", deps + list(scales), d[1], w[1].indirect(so), AF.Copy)]

        vsh = k["own"]
        sh["H"] = pick("H", [vsh], codes=[vp], scales=[ap])
        for b, d in enumerate((ar1, ac1, aS[2], aS[3])):
            free["H", b] = [d]
        la = places("A", [landed(plan[0], "p", "A", t, "cs"), aS[0]], psZ[2], win("A", t, -12, 116))
        lb = places("B", [landed(plan[0], "p", "B", t, "cs"), aS[1]], psZ[3], win("B", t, -12, 116))
        ach = [run("act", [ve], T.chs[0:1, K * t + 16 * m:K * t + 16 * m + 16], psZ[0][0:1, 17 * m + 1:17 * m + 17], AF.Copy)
               for m in range(3)]
        chtok.append(ach[-1])
        if not last:
            decode(t + 1, "h0 h1 h2 h3")
        else:
            store("s", chtok, T.ch[:], T.chs[0:1, :])
            store("s", sh["H"][:1], T.oc[:, 4 * P:8 * P], T.fin[:, P:2 * P].bitcast(dt.uint8))
        if t == 0:
            k_w = quant([lw], cols("wq", 0, 128), T.tw[:])
        vs = {"A": [la()], "B": [lb()]}
        arr = {c: [[landed(plan[1], "r", c, t, "c")], [landed(plan[1], "s", c, t, "s")]] for c in "AB"}
        for b, d in enumerate((ach + [ve], [vsh], vs["A"][:1], vs["B"][:1])):
            free["Z", b] = d
        if last:
            for c in "AB":
                sh[c] = pick(c, vs[c], 0, P, *arr[c])
        else:
            for part, a, b in (("L", 0, L), ("R", L, P)):
                for c in "AB":
                    sh[c + part] = pick(c, vs[c], a, b, *arr[c])
            for c in "AB":
                sh[c] = sh[c + "L"] + sh[c + "R"]
            decode(t + 1, LATER)

    my = mm(sh["A"] + free["Z", 0] + [k_w], psZ[0][:, 0:P], cols("wq", 0, 128), win("A", R, 0, P))
    vy = run("copy", [my], T.yout[:], psZ[0][:, 0:P])
    store("s", sh["A"][:1], T.oc[:, 0:4 * P], T.fin[:, 0:P].bitcast(dt.uint8))
    store("s", sh["B"][:1], T.oc[:, 8 * P:12 * P], T.fin[:, 2 * P:3 * P].bitcast(dt.uint8))
    for j in range(4):
        store("a" if j else "s", sh["A"] + sh["B"] + sh["H"], T.osc[4 * j:4 * j + 4, :], T.fin_s[32 * j:32 * j + 4, :])
    store("s", [vy], T.y[:], T.yout[:])
    wait("g", [("s" + q, c) for q, c in cnt.items()] + list(total.items()))
